import numpy as np
import ml_dtypes


def mxq(x, axis, fmt="e4m3"):
    dtype, down = {"e4m3": (ml_dtypes.float8_e4m3fn, 7), "e5m2": (ml_dtypes.float8_e5m2, 14)}[fmt]
    v = np.moveaxis(np.asarray(x, np.float32).astype(ml_dtypes.bfloat16).astype(np.float64), axis, -1)
    blocks = v.reshape(v.shape[:-1] + (-1, 32))
    amax = np.abs(blocks).max(-1, keepdims=True)
    byte = np.maximum(np.where(amax > 0, np.frexp(amax)[1] - 1 + 127, 0) - down, 1)
    scale = np.exp2(byte - 127.0)
    codes = (blocks / scale).astype(np.float32).astype(dtype).astype(np.float64)
    return np.moveaxis((codes * scale).reshape(v.shape), -1, axis)


WIDE = False


def mx_kscale(k):
    if not WIDE:
        return np.ones(k)
    levels = np.array([10, -10, 5, -5, 0])
    if k % 512:
        return np.exp2(np.random.permutation(np.resize(levels, k // 32))).repeat(32)
    a = np.empty((k // 512, 16))
    for p in range(k // 512):
        a[p, :8] = np.random.permutation(np.resize(levels, 8))
        for g in range(8):
            far = levels[np.abs(levels - a[p, g]) >= 10]
            a[p, g + 8] = far[np.random.randint(len(far))]
    return np.exp2(a.ravel()).repeat(32)


def f64(x):
    return np.asarray(x).astype(np.float64)


def striped(idx):
    return np.tile(np.asarray(idx).reshape(-1, 16).T, (8, 1)).astype(np.uint16)


def unstriped(offs):
    return offs[:16].T.reshape(-1).astype(np.int64)


E2M1 = np.array([0.0, 0.5, 1.0, 1.5, 2.0, 3.0, 4.0, 6.0, -0.0, -0.5, -1.0, -1.5, -2.0, -3.0, -4.0, -6.0])


def pack_weight(w, fmt):
    k, n = w.shape
    w = f64(np.asarray(w, np.float32).astype(ml_dtypes.bfloat16)).reshape(k // 32, 32, n)
    amax = np.abs(w).max(1)
    if fmt == "e4m3":
        byte = np.frexp(amax)[1] - 1 + 127 - 7
    else:
        mant, ex = np.frexp(amax / 6.0)
        byte = np.where(mant > 0.5, ex, ex - 1) + 127
    byte = np.clip(np.where(amax > 0, byte, 1), 1, 254)
    scaled = (w * np.exp2(127.0 - byte)[:, None, :]).reshape(k, n).astype(np.float32)
    by_word = np.ascontiguousarray(scaled.reshape(k // 512, 128, 4, n).transpose(0, 1, 3, 2))
    if fmt == "e4m3":
        words = by_word.astype(ml_dtypes.float8_e4m3fn).view(np.uint8)
    else:
        c = by_word.astype(ml_dtypes.float4_e2m1fn).view(np.uint8) & 0xF
        words = (c[..., 0::2] | (c[..., 1::2] << 4)).reshape(k // 512, 128, 2 * n)
    return np.ascontiguousarray(words), np.ascontiguousarray(byte.astype(np.uint8).reshape(k // 512, 16, n))


def unpack_weight(words, scales, fmt):
    g, _, n = scales.shape
    words = np.ascontiguousarray(words).reshape(g, 128, n, -1)
    if fmt == "e4m3":
        vals = words.view(ml_dtypes.float8_e4m3fn).astype(np.float64)
    else:
        nib = np.empty((g, 128, n, 4), np.uint8)
        nib[..., 0::2] = words & 0xF
        nib[..., 1::2] = words >> 4
        vals = E2M1[nib]
    vals = vals * np.repeat(np.exp2(scales.astype(np.float64) - 127.0), 8, axis=1)[..., None]
    return vals.transpose(0, 1, 3, 2).reshape(g * 512, n)


D, T, I, J, Q = 512, 2048, 512, 256, 128


def setup_inputs():
    n = np.random.standard_normal
    idx = np.random.permutation(T)[:I]
    idx2 = np.random.permutation(T)[:J]
    fd = mx_kscale(D)
    keysp = pack_weight(n((D, T)) / fd[:, None], "e2m1")
    return {
        "query": (n((D, Q)) * 0.6 / np.sqrt(D) * fd[:, None]).astype(np.float32),
        "keys_words": keysp[0],
        "keys_scales": keysp[1],
        "mass": (np.random.uniform(0.0, 2.0, (Q, T))).astype(np.float32),
        "dec": (np.random.uniform(0.8, 1.0, (Q, 1))).astype(np.float32),
        "credit": (np.random.uniform(0.0, 0.5, (1, T))).astype(np.float32),
        "offs": striped(idx),
        "offs2": striped(idx2),
    }


def reference(query, keys_words, keys_scales, mass, dec, credit, offs, offs2):
    idx = unstriped(offs)
    idx2 = unstriped(offs2)
    keysu = unpack_weight(keys_words, keys_scales, "e2m1")
    queryq = mxq(f64(query), 0, "e4m3")
    keysidxg = keysu[:, idx]
    a = queryq.T @ keysidxg
    p = np.exp(a - np.max(a, axis=1, keepdims=True))
    w = p / np.sum(p, axis=1, keepdims=True) * 512.0
    wf = np.zeros((Q, T))
    wf[:, idx] = w
    x = f64(dec) * f64(mass) + wf - f64(credit)
    y = x[:, idx2] * 2.0
    return y

@@ -1,0 +1,158 @@
+from contextlib import ExitStack
+
+import concourse.mybir as mybir
+
+D, T, I, J, Q = 512, 2048, 512, 256, 128
+P = 128
+PACK = 4
+HALVES = 2
+RUN = 8
+GROUP = 4
+
+F32 = mybir.dt.float32
+BF16 = mybir.dt.bfloat16
+I32 = mybir.dt.int32
+U32 = mybir.dt.uint32
+U16 = mybir.dt.uint16
+U8 = mybir.dt.uint8
+FP8X4 = mybir.dt.float8_e4m3fn_x4
+FP4X4 = mybir.dt.float4_e2m1fn_x4
+ALU = mybir.AluOpType
+ACT = mybir.ActivationFunctionType
+
+FLOPS = 2 * D * Q * I
+
+
+def tile_attend_evictscores_kernel(tc, query, keys_words, keys_scales, mass, dec, credit, offs, offs2, out):
+    nc = tc.nc
+    with ExitStack() as ctx:
+        sb = ctx.enter_context(tc.tile_pool(name="sb", bufs=1))
+        score_psum = ctx.enter_context(tc.psum_pool(name="score_psum", bufs=1))
+        credit_psum = ctx.enter_context(tc.psum_pool(name="credit_psum", bufs=2))
+
+        slots = sb.tile([P, I // 16], U16)
+        nc.sync.dma_start(slots[:], offs)
+        credit_cols = sb.tile([P, HALVES, RUN], F32)
+        nc.scalar.dma_start(credit_cols[:], credit.rearrange("o (h p c) -> p (o h) c", h=HALVES, c=RUN))
+        candidates = sb.tile([P, J // 16], U16)
+        nc.sync.dma_start(candidates[:], offs2)
+        word_pool = sb.tile([P, T], U16, align_bytes=64, tag="word_pool")
+        nc.sync.dma_start(word_pool[:].bitcast(I32), keys_words[0].bitcast(I32))
+        query_raw = sb.tile([P, PACK, Q], F32)
+        nc.sync.dma_start(query_raw[:], query.rearrange("(p j) q -> p j q", j=PACK))
+
+        scale_pool = sb.tile([P, T], U8, align_bytes=64)
+        nc.vector.memset(scale_pool[:].bitcast(I32), 0)
+        for quad in range(4):
+            nc.scalar.dma_start(
+                scale_pool[32 * quad : 32 * quad + 4, :].bitcast(I32),
+                keys_scales[0, 4 * quad : 4 * quad + 4, :].bitcast(I32),
+            )
+        warm_in = sb.tile([P, 1], F32)
+        nc.gpsimd.memset(warm_in[:], 0.0)
+        warm_out = sb.tile([P, 1], F32)
+        nc.scalar.activation(warm_out[:], warm_in[:], ACT.Exp)
+
+        ones = sb.tile([P, P], F32, tag="late")
+        nc.vector.memset(ones[:], 1.0)
+        identity = sb.tile([P, P], F32)
+        nc.gpsimd.affine_select(
+            out=identity[:],
+            in_=ones[:],
+            pattern=[[-1, P]],
+            compare_op=ALU.is_equal,
+            fill=0.0,
+            base=0,
+            channel_multiplier=1,
+        )
+        placed = sb.tile([P, T], F32)
+        nc.vector.memset(placed[:], 0.0)
+
+        late = sb.tile([P, T + RUN], F32, tag="late")
+        decay = late[:, T : T + 1]
+        mass_halves = [late[:, h * (T // HALVES) : (h + 1) * (T // HALVES)] for h in range(HALVES)]
+        nc.sync.dma_start(mass_halves[0], mass[:, : T // HALVES])
+        nc.sync.dma_start(decay, dec)
+        nc.sync.dma_start(mass_halves[1], mass[:, T // HALVES :])
+
+        credit_flat = credit_cols[:].rearrange("p h c -> p (h c)")
+        credit2_first = sb.tile([P, GROUP], F32, align_bytes=64, tag="credit2_first")
+        nc.gpsimd.tensor_scalar(credit2_first[:], credit_flat[:, :GROUP], 2.0, 0.0, ALU.mult, ALU.add)
+        credit2_rest = sb.tile([P, HALVES * RUN - GROUP], F32)
+        nc.gpsimd.tensor_scalar(credit2_rest[:], credit_flat[:, GROUP:], 2.0, 0.0, ALU.mult, ALU.add)
+        credit2_cols = [credit2_first[:, c : c + 1] for c in range(GROUP)]
+        credit2_cols.extend(credit2_rest[:, c : c + 1] for c in range(HALVES * RUN - GROUP))
+        decay2_first = sb.tile([P, 1], F32, tag="decay2_first")
+        nc.gpsimd.tensor_scalar(decay2_first[:], decay, 2.0, 0.0, ALU.mult, ALU.add)
+        decay2 = sb.tile([P, 1], F32)
+        nc.gpsimd.tensor_scalar(decay2[:], decay, 2.0, 0.0, ALU.mult, ALU.add)
+
+        def spread_credit(h, g):
+            bank = credit_psum.tile([P, GROUP, P], F32, name="credit_bank")
+            for i in range(GROUP):
+                column = credit2_cols[h * RUN + g * GROUP + i]
+                nc.tensor.transpose(bank[:, i, :], column.to_broadcast([P, P]), identity[:])
+            return bank
+
+        first_bank = spread_credit(0, 0)
+
+        key_words = sb.tile([P, I], U16, align_bytes=64)
+        nc.vector.tensor_copy(key_words[:], word_pool[:].indirect(slots[:]))
+
+        query_bf = sb.tile([P, Q, PACK], BF16, align_bytes=64, tag="query_bf")
+        nc.scalar.copy(query_bf[:], query_raw[:].rearrange("p j q -> p q j"))
+        query_codes = sb.tile([P, Q], U32, align_bytes=64, tag="word_pool")
+        query_scales = sb.tile([P, Q], U8, align_bytes=64, tag="credit2_first")
+        nc.vector.quantize_mx(
+            out=query_codes[:].bitcast(FP8X4),
+            scales=query_scales[:],
+            in_=query_bf[:].rearrange("p q j -> p (q j)"),
+        )
+
+        key_scales = sb.tile([P, I], U8, align_bytes=64, tag="query_bf")
+        nc.vector.tensor_copy(key_scales[:], scale_pool[:].indirect(slots[:]))
+
+        base = sb.tile([P, T], F32)
+
+        def base_part(h, g, bank, factor):
+            cols = slice(g * GROUP, (g + 1) * GROUP)
+            base_half = base[:, h * (T // HALVES) : (h + 1) * (T // HALVES)]
+            nc.vector.scalar_tensor_tensor(
+                base_half.rearrange("p (k c) -> p k c", c=RUN)[:, :, cols],
+                mass_halves[h].rearrange("p (k c) -> p k c", c=RUN)[:, :, cols],
+                factor[:],
+                bank[:].rearrange("p i k -> p k i"),
+                ALU.mult,
+                ALU.subtract,
+            )
+
+        scores = score_psum.tile([P, I], F32)
+        nc.tensor.matmul_mx(
+            out=scores[:],
+            lhsT=query_codes[:].bitcast(FP8X4),
+            lhsT_scale=query_scales[:],
+            rhs=key_words[:].bitcast(FP4X4),
+            rhs_scale=key_scales[:],
+            start=True,
+            stop=True,
+        )
+        base_part(0, 0, first_bank, decay2_first)
+        neg_max = sb.tile([P, 1], F32, tag="decay2_first")
+        nc.vector.tensor_reduce(neg_max[:], scores[:], mybir.AxisListType.X, ALU.max, negate=True)
+        weights = sb.tile([P, I], F32)
+        row_sum = sb.tile([P, 1], F32)
+        nc.scalar.activation(weights[:], scores[:], ACT.Exp, bias=neg_max[:], accum_out=row_sum[:])
+        base_part(0, 1, spread_credit(0, 1), decay2)
+        nc.vector.tensor_copy(placed[:].indirect(slots[:]), weights[:])
+        row_sum_scaled = sb.tile([P, 1], F32)
+        nc.scalar.mul(row_sum_scaled[:], row_sum[:], 1.0 / 1024.0)
+        row_factor = sb.tile([P, 1], F32)
+        nc.vector.reciprocal(row_factor[:], row_sum_scaled[:])
+        base_part(1, 0, spread_credit(1, 0), decay2)
+        base_part(1, 1, spread_credit(1, 1), decay2)
+
+        updated = sb.tile([P, T], F32)
+        nc.vector.scalar_tensor_tensor(updated[:], placed[:], row_factor[:], base[:], ALU.mult, ALU.add)
+        picked = sb.tile([P, J], F32)
+        nc.vector.tensor_copy(picked[:], updated[:].indirect(candidates[:]))
+        nc.sync.dma_start(out, picked[:])

@@ -5,9 +5,9 @@ import concourse.mybir as mybir
 D, T, I, J, Q = 512, 2048, 512, 256, 128
 P = 128
 PACK = 4
-HALVES = 2
-RUN = 8
-GROUP = 4
+BANK = 512
+BLOCKS = BANK // P
+HALF = T // 2
 
 F32 = mybir.dt.float32
 BF16 = mybir.dt.bfloat16
@@ -28,12 +28,10 @@ def tile_attend_evictscores_kernel(tc, query, keys_words, keys_scales, mass, dec
     with ExitStack() as ctx:
         sb = ctx.enter_context(tc.tile_pool(name="sb", bufs=1))
         score_psum = ctx.enter_context(tc.psum_pool(name="score_psum", bufs=1))
-        credit_psum = ctx.enter_context(tc.psum_pool(name="credit_psum", bufs=2))
+        pair_psum = ctx.enter_context(tc.psum_pool(name="pair_psum", bufs=2))
 
         slots = sb.tile([P, I // 16], U16)
         nc.sync.dma_start(slots[:], offs)
-        credit_cols = sb.tile([P, HALVES, RUN], F32)
-        nc.scalar.dma_start(credit_cols[:], credit.rearrange("o (h p c) -> p (o h) c", h=HALVES, c=RUN))
         candidates = sb.tile([P, J // 16], U16)
         nc.sync.dma_start(candidates[:], offs2)
         word_pool = sb.tile([P, T], U16, align_bytes=64, tag="word_pool")
@@ -41,17 +39,21 @@ def tile_attend_evictscores_kernel(tc, query, keys_words, keys_scales, mass, dec
         query_raw = sb.tile([P, PACK, Q], F32)
         nc.sync.dma_start(query_raw[:], query.rearrange("(p j) q -> p j q", j=PACK))
 
-        scale_pool = sb.tile([P, T], U8, align_bytes=64)
-        nc.vector.memset(scale_pool[:].bitcast(I32), 0)
-        for quad in range(4):
-            nc.scalar.dma_start(
-                scale_pool[32 * quad : 32 * quad + 4, :].bitcast(I32),
-                keys_scales[0, 4 * quad : 4 * quad + 4, :].bitcast(I32),
-            )
+        credit_rows = sb.tile([P, P], F32)
+        nc.gpsimd.memset(credit_rows[:], 0.0)
+        nc.scalar.dma_start(credit_rows[: T // P, :], credit.rearrange("o (c p) -> (o c) p", p=P))
         warm_in = sb.tile([P, 1], F32)
         nc.gpsimd.memset(warm_in[:], 0.0)
         warm_out = sb.tile([P, 1], F32)
         nc.scalar.activation(warm_out[:], warm_in[:], ACT.Exp)
+
+        scale_pool = sb.tile([P, T], U8, align_bytes=64)
+        nc.vector.memset(scale_pool[:].bitcast(I32), 0)
+        for quad in range(4):
+            nc.sync.dma_start(
+                scale_pool[32 * quad : 32 * quad + 4, :].bitcast(I32),
+                keys_scales[0, 4 * quad : 4 * quad + 4, :].bitcast(I32),
+            )
 
         ones = sb.tile([P, P], F32, tag="late")
         nc.vector.memset(ones[:], 1.0)
@@ -68,63 +70,59 @@ def tile_attend_evictscores_kernel(tc, query, keys_words, keys_scales, mass, dec
         placed = sb.tile([P, T], F32)
         nc.vector.memset(placed[:], 0.0)
 
-        late = sb.tile([P, T + RUN], F32, tag="late")
+        late = sb.tile([P, T + 1], F32, tag="late")
         decay = late[:, T : T + 1]
-        mass_halves = [late[:, h * (T // HALVES) : (h + 1) * (T // HALVES)] for h in range(HALVES)]
-        nc.sync.dma_start(mass_halves[0], mass[:, : T // HALVES])
-        nc.sync.dma_start(decay, dec)
-        nc.sync.dma_start(mass_halves[1], mass[:, T // HALVES :])
+        nc.gpsimd.dma_start(decay, dec)
+        nc.sync.dma_start(late[:, :HALF], mass[:, :HALF])
+        nc.sync.dma_start(late[:, HALF:T], mass[:, HALF:])
 
-        credit_flat = credit_cols[:].rearrange("p h c -> p (h c)")
-        credit2_first = sb.tile([P, GROUP], F32, align_bytes=64, tag="credit2_first")
-        nc.gpsimd.tensor_scalar(credit2_first[:], credit_flat[:, :GROUP], 2.0, 0.0, ALU.mult, ALU.add)
-        credit2_rest = sb.tile([P, HALVES * RUN - GROUP], F32)
-        nc.gpsimd.tensor_scalar(credit2_rest[:], credit_flat[:, GROUP:], 2.0, 0.0, ALU.mult, ALU.add)
-        credit2_cols = [credit2_first[:, c : c + 1] for c in range(GROUP)]
-        credit2_cols.extend(credit2_rest[:, c : c + 1] for c in range(HALVES * RUN - GROUP))
         decay2_first = sb.tile([P, 1], F32, tag="decay2_first")
         nc.gpsimd.tensor_scalar(decay2_first[:], decay, 2.0, 0.0, ALU.mult, ALU.add)
         decay2 = sb.tile([P, 1], F32)
         nc.gpsimd.tensor_scalar(decay2[:], decay, 2.0, 0.0, ALU.mult, ALU.add)
 
-        def spread_credit(h, g):
-            bank = credit_psum.tile([P, GROUP, P], F32, name="credit_bank")
-            for i in range(GROUP):
-                column = credit2_cols[h * RUN + g * GROUP + i]
-                nc.tensor.transpose(bank[:, i, :], column.to_broadcast([P, P]), identity[:])
+        credit_turned = score_psum.tile([P, P], F32)
+        nc.tensor.transpose(credit_turned[:], credit_rows[:], identity[:])
+        debit_first = sb.tile([P, BLOCKS], F32, align_bytes=64, tag="debit_first")
+        nc.scalar.mul(debit_first[:], credit_turned[:, :BLOCKS], -2.0)
+        debit_rest = sb.tile([P, T // P - BLOCKS], F32)
+        nc.scalar.mul(debit_rest[:], credit_turned[:, BLOCKS : T // P], -2.0)
+        debit_cols = [debit_first[:, c : c + 1] for c in range(BLOCKS)]
+        debit_cols.extend(debit_rest[:, c : c + 1] for c in range(T // P - BLOCKS))
+
+        def spread_debit(quarter):
+            bank = score_psum.tile([P, BANK], F32, name="debit_bank")
+            for i in range(BLOCKS):
+                column = debit_cols[quarter * BLOCKS + i]
+                nc.tensor.transpose(bank[:, i * P : (i + 1) * P], column.to_broadcast([P, P]), identity[:])
             return bank
 
-        first_bank = spread_credit(0, 0)
+        first_bank = spread_debit(0)
 
         key_words = sb.tile([P, I], U16, align_bytes=64)
         nc.vector.tensor_copy(key_words[:], word_pool[:].indirect(slots[:]))
 
-        query_bf = sb.tile([P, Q, PACK], BF16, align_bytes=64, tag="query_bf")
-        nc.scalar.copy(query_bf[:], query_raw[:].rearrange("p j q -> p q j"))
+        query_bf = sb.tile([P, Q, PACK], BF16, align_bytes=64)
+        nc.scalar.copy(
+            query_bf[:].rearrange("p (c i) j -> p c j i", i=PACK),
+            query_raw[:].rearrange("p j (c i) -> p c j i", i=PACK),
+        )
         query_codes = sb.tile([P, Q], U32, align_bytes=64, tag="word_pool")
-        query_scales = sb.tile([P, Q], U8, align_bytes=64, tag="credit2_first")
+        query_scales = sb.tile([P, Q], U8, align_bytes=64)
         nc.vector.quantize_mx(
             out=query_codes[:].bitcast(FP8X4),
             scales=query_scales[:],
             in_=query_bf[:].rearrange("p q j -> p (q j)"),
         )
 
-        key_scales = sb.tile([P, I], U8, align_bytes=64, tag="query_bf")
+        key_scales = sb.tile([P, I], U8, align_bytes=64, tag="debit_first")
         nc.vector.tensor_copy(key_scales[:], scale_pool[:].indirect(slots[:]))
 
-        base = sb.tile([P, T], F32)
+        base = sb.tile([P, HALF], F32)
 
-        def base_part(h, g, bank, factor):
-            cols = slice(g * GROUP, (g + 1) * GROUP)
-            base_half = base[:, h * (T // HALVES) : (h + 1) * (T // HALVES)]
-            nc.vector.scalar_tensor_tensor(
-                base_half.rearrange("p (k c) -> p k c", c=RUN)[:, :, cols],
-                mass_halves[h].rearrange("p (k c) -> p k c", c=RUN)[:, :, cols],
-                factor[:],
-                bank[:].rearrange("p i k -> p k i"),
-                ALU.mult,
-                ALU.subtract,
-            )
+        def base_on_vector(quarter, bank, factor):
+            cols = slice(quarter * BANK, (quarter + 1) * BANK)
+            nc.vector.scalar_tensor_tensor(base[:, cols], late[:, cols], factor[:], bank[:], ALU.mult, ALU.add)
 
         scores = score_psum.tile([P, I], F32)
         nc.tensor.matmul_mx(
@@ -136,23 +134,55 @@ def tile_attend_evictscores_kernel(tc, query, keys_words, keys_scales, mass, dec
             start=True,
             stop=True,
         )
-        base_part(0, 0, first_bank, decay2_first)
+        base_on_vector(0, first_bank, decay2_first)
         neg_max = sb.tile([P, 1], F32, tag="decay2_first")
         nc.vector.tensor_reduce(neg_max[:], scores[:], mybir.AxisListType.X, ALU.max, negate=True)
         weights = sb.tile([P, I], F32)
         row_sum = sb.tile([P, 1], F32)
         nc.scalar.activation(weights[:], scores[:], ACT.Exp, bias=neg_max[:], accum_out=row_sum[:])
-        base_part(0, 1, spread_credit(0, 1), decay2)
+        base_on_vector(1, spread_debit(1), decay2)
         nc.vector.tensor_copy(placed[:].indirect(slots[:]), weights[:])
         row_sum_scaled = sb.tile([P, 1], F32)
         nc.scalar.mul(row_sum_scaled[:], row_sum[:], 1.0 / 1024.0)
         row_factor = sb.tile([P, 1], F32)
         nc.vector.reciprocal(row_factor[:], row_sum_scaled[:])
-        base_part(1, 0, spread_credit(1, 0), decay2)
-        base_part(1, 1, spread_credit(1, 1), decay2)
+
+        decayed = sb.tile([P, HALF], F32, tag="decay2_first")
+        turned_banks = []
+        for j in range(2):
+            cols = slice(j * BANK, (j + 1) * BANK)
+            nc.scalar.mul(decayed[:, cols], late[:, HALF + j * BANK : HALF + (j + 1) * BANK], decay2[:])
+            bank = pair_psum.tile([P, BANK], F32, name="turned_bank")
+            for i in range(BLOCKS):
+                block = slice(j * BANK + i * P, j * BANK + (i + 1) * P)
+                nc.tensor.transpose(bank[:, i * P : (i + 1) * P], decayed[:, block], identity[:])
+            turned_banks.append(bank)
+        base_turned = sb.tile([P, HALF], F32)
+        base_banks = []
+        for j in range(2):
+            bank = pair_psum.tile([P, BANK], F32, name="base_bank")
+            for i in range(BLOCKS):
+                block = slice(j * BANK + i * P, j * BANK + (i + 1) * P)
+                nc.scalar.activation(
+                    base_turned[:, block],
+                    turned_banks[j][:, i * P : (i + 1) * P],
+                    ACT.Identity,
+                    bias=debit_cols[(2 + j) * BLOCKS + i],
+                )
+            for i in range(BLOCKS):
+                block = slice(j * BANK + i * P, j * BANK + (i + 1) * P)
+                nc.tensor.transpose(bank[:, i * P : (i + 1) * P], base_turned[:, block], identity[:])
+            base_banks.append(bank)
 
         updated = sb.tile([P, T], F32)
-        nc.vector.scalar_tensor_tensor(updated[:], placed[:], row_factor[:], base[:], ALU.mult, ALU.add)
+        nc.vector.scalar_tensor_tensor(
+            updated[:, :HALF], placed[:, :HALF], row_factor[:], base[:], ALU.mult, ALU.add
+        )
+        for j in range(2):
+            cols = slice(HALF + j * BANK, HALF + (j + 1) * BANK)
+            nc.vector.scalar_tensor_tensor(
+                updated[:, cols], placed[:, cols], row_factor[:], base_banks[j][:], ALU.mult, ALU.add
+            )
         picked = sb.tile([P, J], F32)
         nc.vector.tensor_copy(picked[:], updated[:].indirect(candidates[:]))
         nc.sync.dma_start(out, picked[:])

@@ -32,20 +32,21 @@ def tile_attend_evictscores_kernel(tc, query, keys_words, keys_scales, mass, dec
 
         slots = sb.tile([P, I // 16], U16)
         nc.sync.dma_start(slots[:], offs)
+        credit_rows = sb.tile([P, P], F32)
+        nc.scalar.dma_start(credit_rows[P - T // P :, :], credit.rearrange("o (c p) -> (o c) p", p=P))
+        warm_in = sb.tile([P, 1], F32)
+        nc.gpsimd.memset(warm_in[:], 0.0)
+        warm_out = sb.tile([P, 1], F32)
+        nc.scalar.activation(warm_out[:], warm_in[:], ACT.Exp)
+        nc.gpsimd.memset(credit_rows[: P - T // P, :], 0.0)
+        minus_two = sb.tile([P, 1], F32, align_bytes=64, tag="query_bf")
+        nc.gpsimd.memset(minus_two[:], -2.0)
         candidates = sb.tile([P, J // 16], U16)
         nc.sync.dma_start(candidates[:], offs2)
         word_pool = sb.tile([P, T], U16, align_bytes=64, tag="word_pool")
         nc.sync.dma_start(word_pool[:].bitcast(I32), keys_words[0].bitcast(I32))
         query_raw = sb.tile([P, PACK, Q], F32)
         nc.sync.dma_start(query_raw[:], query.rearrange("(p j) q -> p j q", j=PACK))
-
-        credit_rows = sb.tile([P, P], F32)
-        nc.gpsimd.memset(credit_rows[:], 0.0)
-        nc.scalar.dma_start(credit_rows[: T // P, :], credit.rearrange("o (c p) -> (o c) p", p=P))
-        warm_in = sb.tile([P, 1], F32)
-        nc.gpsimd.memset(warm_in[:], 0.0)
-        warm_out = sb.tile([P, 1], F32)
-        nc.scalar.activation(warm_out[:], warm_in[:], ACT.Exp)
 
         scale_pool = sb.tile([P, T], U8, align_bytes=64)
         nc.vector.memset(scale_pool[:].bitcast(I32), 0)
@@ -72,26 +73,21 @@ def tile_attend_evictscores_kernel(tc, query, keys_words, keys_scales, mass, dec
 
         late = sb.tile([P, T + 1], F32, tag="late")
         decay = late[:, T : T + 1]
-        nc.gpsimd.dma_start(decay, dec)
+        nc.sync.dma_start(decay, dec)
         nc.sync.dma_start(late[:, :HALF], mass[:, :HALF])
         nc.sync.dma_start(late[:, HALF:T], mass[:, HALF:])
-
-        decay2_first = sb.tile([P, 1], F32, tag="decay2_first")
-        nc.gpsimd.tensor_scalar(decay2_first[:], decay, 2.0, 0.0, ALU.mult, ALU.add)
-        decay2 = sb.tile([P, 1], F32)
-        nc.gpsimd.tensor_scalar(decay2[:], decay, 2.0, 0.0, ALU.mult, ALU.add)
 
         credit_turned = score_psum.tile([P, P], F32)
         nc.tensor.transpose(credit_turned[:], credit_rows[:], identity[:])
         debit_first = sb.tile([P, BLOCKS], F32, align_bytes=64, tag="debit_first")
-        nc.scalar.mul(debit_first[:], credit_turned[:, :BLOCKS], -2.0)
+        nc.scalar.mul(debit_first[:], credit_turned[:, P - T // P : P - T // P + BLOCKS], minus_two[:])
         debit_rest = sb.tile([P, T // P - BLOCKS], F32)
-        nc.scalar.mul(debit_rest[:], credit_turned[:, BLOCKS : T // P], -2.0)
+        nc.scalar.mul(debit_rest[:], credit_turned[:, P - T // P + BLOCKS :], minus_two[:])
         debit_cols = [debit_first[:, c : c + 1] for c in range(BLOCKS)]
         debit_cols.extend(debit_rest[:, c : c + 1] for c in range(T // P - BLOCKS))
 
         def spread_debit(quarter):
-            bank = score_psum.tile([P, BANK], F32, name="debit_bank")
+            bank = pair_psum.tile([P, BANK], F32, name="debit_bank")
             for i in range(BLOCKS):
                 column = debit_cols[quarter * BLOCKS + i]
                 nc.tensor.transpose(bank[:, i * P : (i + 1) * P], column.to_broadcast([P, P]), identity[:])
@@ -102,44 +98,56 @@ def tile_attend_evictscores_kernel(tc, query, keys_words, keys_scales, mass, dec
         key_words = sb.tile([P, I], U16, align_bytes=64)
         nc.vector.tensor_copy(key_words[:], word_pool[:].indirect(slots[:]))
 
-        query_bf = sb.tile([P, Q, PACK], BF16, align_bytes=64)
+        key_scales_lo = sb.tile([P, I // 2], U8, align_bytes=64)
+        nc.vector.tensor_copy(key_scales_lo[:], scale_pool[:].indirect(slots[:, : I // 32]))
+
+        query_bf = sb.tile([P, Q, PACK], BF16, align_bytes=64, tag="query_bf")
         nc.scalar.copy(
             query_bf[:].rearrange("p (c i) j -> p c j i", i=PACK),
             query_raw[:].rearrange("p j (c i) -> p c j i", i=PACK),
         )
         query_codes = sb.tile([P, Q], U32, align_bytes=64, tag="word_pool")
-        query_scales = sb.tile([P, Q], U8, align_bytes=64)
+        query_scales = sb.tile([P, Q], U8, align_bytes=64, tag="debit_first")
         nc.vector.quantize_mx(
             out=query_codes[:].bitcast(FP8X4),
             scales=query_scales[:],
             in_=query_bf[:].rearrange("p q j -> p (q j)"),
         )
 
-        key_scales = sb.tile([P, I], U8, align_bytes=64, tag="debit_first")
-        nc.vector.tensor_copy(key_scales[:], scale_pool[:].indirect(slots[:]))
+        key_scales_hi = sb.tile([P, I // 2], U8, align_bytes=64, tag="query_bf")
+        nc.vector.tensor_copy(key_scales_hi[:], scale_pool[:].indirect(slots[:, I // 32 :]))
 
+        decay2_first = sb.tile([P, 1], F32, tag="decay2_first")
+        nc.scalar.mul(decay2_first[:], decay, 2.0)
+        decay2 = sb.tile([P, 1], F32)
+        nc.scalar.mul(decay2[:], decay, 2.0)
         base = sb.tile([P, HALF], F32)
+        minus_one = base[:, HALF - 1 : HALF]
+        nc.gpsimd.memset(minus_one, -1.0)
 
         def base_on_vector(quarter, bank, factor):
             cols = slice(quarter * BANK, (quarter + 1) * BANK)
             nc.vector.scalar_tensor_tensor(base[:, cols], late[:, cols], factor[:], bank[:], ALU.mult, ALU.add)
 
         scores = score_psum.tile([P, I], F32)
-        nc.tensor.matmul_mx(
-            out=scores[:],
-            lhsT=query_codes[:].bitcast(FP8X4),
-            lhsT_scale=query_scales[:],
-            rhs=key_words[:].bitcast(FP4X4),
-            rhs_scale=key_scales[:],
-            start=True,
-            stop=True,
-        )
+        for half, key_scales in enumerate((key_scales_lo, key_scales_hi)):
+            cols = slice(half * (I // 2), (half + 1) * (I // 2))
+            nc.tensor.matmul_mx(
+                out=scores[:, cols],
+                lhsT=query_codes[:].bitcast(FP8X4),
+                lhsT_scale=query_scales[:],
+                rhs=key_words[:, cols].bitcast(FP4X4),
+                rhs_scale=key_scales[:],
+                start=True,
+                stop=True,
+            )
         base_on_vector(0, first_bank, decay2_first)
         neg_max = sb.tile([P, 1], F32, tag="decay2_first")
-        nc.vector.tensor_reduce(neg_max[:], scores[:], mybir.AxisListType.X, ALU.max, negate=True)
+        neg_scores = sb.tile([P, I], F32)
+        nc.vector.tensor_scalar(neg_scores[:], scores[:], minus_one, None, ALU.mult, ALU.min, accum_out=neg_max[:])
         weights = sb.tile([P, I], F32)
         row_sum = sb.tile([P, 1], F32)
-        nc.scalar.activation(weights[:], scores[:], ACT.Exp, bias=neg_max[:], accum_out=row_sum[:])
+        nc.scalar.activation(weights[:], neg_scores[:], ACT.Exp, bias=neg_max[:], scale=-1.0, accum_out=row_sum[:])
         base_on_vector(1, spread_debit(1), decay2)
         nc.vector.tensor_copy(placed[:].indirect(slots[:]), weights[:])
         row_sum_scaled = sb.tile([P, 1], F32)

@@ -5,9 +5,17 @@ import concourse.mybir as mybir
 D, T, I, J, Q = 512, 2048, 512, 256, 128
 P = 128
 PACK = 4
+LIST_ROWS = 16
+QUADRANT = 32
+SCALE_ROWS = 4
 BANK = 512
 BLOCKS = BANK // P
 HALF = T // 2
+VECTOR_QUARTERS = HALF // BANK
+TURNED_QUARTERS = (T - HALF) // BANK
+CREDIT_ROWS = T // P
+FIRST_CREDIT_ROW = P - CREDIT_ROWS
+WEIGHT_SCALE = 2.0 * 512.0
 
 F32 = mybir.dt.float32
 BF16 = mybir.dt.bfloat16
@@ -30,18 +38,16 @@ def tile_attend_evictscores_kernel(tc, query, keys_words, keys_scales, mass, dec
         score_psum = ctx.enter_context(tc.psum_pool(name="score_psum", bufs=1))
         pair_psum = ctx.enter_context(tc.psum_pool(name="pair_psum", bufs=2))
 
-        slots = sb.tile([P, I // 16], U16)
+        slots = sb.tile([P, I // LIST_ROWS], U16)
         nc.sync.dma_start(slots[:], offs)
+
         credit_rows = sb.tile([P, P], F32)
-        nc.scalar.dma_start(credit_rows[P - T // P :, :], credit.rearrange("o (c p) -> (o c) p", p=P))
-        warm_in = sb.tile([P, 1], F32)
-        nc.gpsimd.memset(warm_in[:], 0.0)
-        warm_out = sb.tile([P, 1], F32)
-        nc.scalar.activation(warm_out[:], warm_in[:], ACT.Exp)
-        nc.gpsimd.memset(credit_rows[: P - T // P, :], 0.0)
+        nc.scalar.dma_start(credit_rows[FIRST_CREDIT_ROW:, :], credit.rearrange("o (c p) -> (o c) p", p=P))
+        nc.gpsimd.memset(credit_rows[:FIRST_CREDIT_ROW, :], 0.0)
         minus_two = sb.tile([P, 1], F32, align_bytes=64, tag="query_bf")
         nc.gpsimd.memset(minus_two[:], -2.0)
-        candidates = sb.tile([P, J // 16], U16)
+
+        candidates = sb.tile([P, J // LIST_ROWS], U16)
         nc.sync.dma_start(candidates[:], offs2)
         word_pool = sb.tile([P, T], U16, align_bytes=64, tag="word_pool")
         nc.sync.dma_start(word_pool[:].bitcast(I32), keys_words[0].bitcast(I32))
@@ -50,10 +56,10 @@ def tile_attend_evictscores_kernel(tc, query, keys_words, keys_scales, mass, dec
 
         scale_pool = sb.tile([P, T], U8, align_bytes=64)
         nc.vector.memset(scale_pool[:].bitcast(I32), 0)
-        for quad in range(4):
+        for quad in range(P // QUADRANT):
             nc.sync.dma_start(
-                scale_pool[32 * quad : 32 * quad + 4, :].bitcast(I32),
-                keys_scales[0, 4 * quad : 4 * quad + 4, :].bitcast(I32),
+                scale_pool[QUADRANT * quad : QUADRANT * quad + SCALE_ROWS, :].bitcast(I32),
+                keys_scales[0, SCALE_ROWS * quad : SCALE_ROWS * (quad + 1), :].bitcast(I32),
             )
 
         ones = sb.tile([P, P], F32, tag="late")
@@ -80,26 +86,27 @@ def tile_attend_evictscores_kernel(tc, query, keys_words, keys_scales, mass, dec
         credit_turned = score_psum.tile([P, P], F32)
         nc.tensor.transpose(credit_turned[:], credit_rows[:], identity[:])
         debit_first = sb.tile([P, BLOCKS], F32, align_bytes=64, tag="debit_first")
-        nc.scalar.mul(debit_first[:], credit_turned[:, P - T // P : P - T // P + BLOCKS], minus_two[:])
-        debit_rest = sb.tile([P, T // P - BLOCKS], F32)
-        nc.scalar.mul(debit_rest[:], credit_turned[:, P - T // P + BLOCKS :], minus_two[:])
+        nc.scalar.mul(debit_first[:], credit_turned[:, FIRST_CREDIT_ROW : FIRST_CREDIT_ROW + BLOCKS], minus_two[:])
+        debit_rest = sb.tile([P, CREDIT_ROWS - BLOCKS], F32)
+        nc.scalar.mul(debit_rest[:], credit_turned[:, FIRST_CREDIT_ROW + BLOCKS :], minus_two[:])
         debit_cols = [debit_first[:, c : c + 1] for c in range(BLOCKS)]
-        debit_cols.extend(debit_rest[:, c : c + 1] for c in range(T // P - BLOCKS))
+        debit_cols.extend(debit_rest[:, c : c + 1] for c in range(CREDIT_ROWS - BLOCKS))
 
         def spread_debit(quarter):
-            bank = pair_psum.tile([P, BANK], F32, name="debit_bank")
+            debit_bank = pair_psum.tile([P, BANK], F32, name="debit_bank")
             for i in range(BLOCKS):
                 column = debit_cols[quarter * BLOCKS + i]
-                nc.tensor.transpose(bank[:, i * P : (i + 1) * P], column.to_broadcast([P, P]), identity[:])
-            return bank
+                nc.tensor.transpose(debit_bank[:, i * P : (i + 1) * P], column.to_broadcast([P, P]), identity[:])
+            return debit_bank
 
-        first_bank = spread_debit(0)
+        first_debit_bank = spread_debit(0)
 
         key_words = sb.tile([P, I], U16, align_bytes=64)
         nc.vector.tensor_copy(key_words[:], word_pool[:].indirect(slots[:]))
 
+        half_list = I // 2 // LIST_ROWS
         key_scales_lo = sb.tile([P, I // 2], U8, align_bytes=64)
-        nc.vector.tensor_copy(key_scales_lo[:], scale_pool[:].indirect(slots[:, : I // 32]))
+        nc.vector.tensor_copy(key_scales_lo[:], scale_pool[:].indirect(slots[:, :half_list]))
 
         query_bf = sb.tile([P, Q, PACK], BF16, align_bytes=64, tag="query_bf")
         nc.scalar.copy(
@@ -115,7 +122,7 @@ def tile_attend_evictscores_kernel(tc, query, keys_words, keys_scales, mass, dec
         )
 
         key_scales_hi = sb.tile([P, I // 2], U8, align_bytes=64, tag="query_bf")
-        nc.vector.tensor_copy(key_scales_hi[:], scale_pool[:].indirect(slots[:, I // 32 :]))
+        nc.vector.tensor_copy(key_scales_hi[:], scale_pool[:].indirect(slots[:, half_list:]))
 
         decay2_first = sb.tile([P, 1], F32, tag="decay2_first")
         nc.scalar.mul(decay2_first[:], decay, 2.0)
@@ -125,23 +132,25 @@ def tile_attend_evictscores_kernel(tc, query, keys_words, keys_scales, mass, dec
         minus_one = base[:, HALF - 1 : HALF]
         nc.gpsimd.memset(minus_one, -1.0)
 
-        def base_on_vector(quarter, bank, factor):
+        def base_on_vector(quarter, debit_bank, doubled_decay):
             cols = slice(quarter * BANK, (quarter + 1) * BANK)
-            nc.vector.scalar_tensor_tensor(base[:, cols], late[:, cols], factor[:], bank[:], ALU.mult, ALU.add)
+            nc.vector.scalar_tensor_tensor(
+                base[:, cols], late[:, cols], doubled_decay[:], debit_bank[:], ALU.mult, ALU.add
+            )
 
         scores = score_psum.tile([P, I], F32)
         for half, key_scales in enumerate((key_scales_lo, key_scales_hi)):
-            cols = slice(half * (I // 2), (half + 1) * (I // 2))
+            half_slots = slice(half * (I // 2), (half + 1) * (I // 2))
             nc.tensor.matmul_mx(
-                out=scores[:, cols],
+                out=scores[:, half_slots],
                 lhsT=query_codes[:].bitcast(FP8X4),
                 lhsT_scale=query_scales[:],
-                rhs=key_words[:, cols].bitcast(FP4X4),
+                rhs=key_words[:, half_slots].bitcast(FP4X4),
                 rhs_scale=key_scales[:],
                 start=True,
                 stop=True,
             )
-        base_on_vector(0, first_bank, decay2_first)
+        base_on_vector(0, first_debit_bank, decay2_first)
         neg_max = sb.tile([P, 1], F32, tag="decay2_first")
         neg_scores = sb.tile([P, I], F32)
         nc.vector.tensor_scalar(neg_scores[:], scores[:], minus_one, None, ALU.mult, ALU.min, accum_out=neg_max[:])
@@ -151,42 +160,42 @@ def tile_attend_evictscores_kernel(tc, query, keys_words, keys_scales, mass, dec
         base_on_vector(1, spread_debit(1), decay2)
         nc.vector.tensor_copy(placed[:].indirect(slots[:]), weights[:])
         row_sum_scaled = sb.tile([P, 1], F32)
-        nc.scalar.mul(row_sum_scaled[:], row_sum[:], 1.0 / 1024.0)
+        nc.scalar.mul(row_sum_scaled[:], row_sum[:], 1.0 / WEIGHT_SCALE)
         row_factor = sb.tile([P, 1], F32)
         nc.vector.reciprocal(row_factor[:], row_sum_scaled[:])
 
         decayed = sb.tile([P, HALF], F32, tag="decay2_first")
         turned_banks = []
-        for j in range(2):
+        for j in range(TURNED_QUARTERS):
             cols = slice(j * BANK, (j + 1) * BANK)
             nc.scalar.mul(decayed[:, cols], late[:, HALF + j * BANK : HALF + (j + 1) * BANK], decay2[:])
-            bank = pair_psum.tile([P, BANK], F32, name="turned_bank")
+            turned_bank = pair_psum.tile([P, BANK], F32, name="turned_bank")
             for i in range(BLOCKS):
                 block = slice(j * BANK + i * P, j * BANK + (i + 1) * P)
-                nc.tensor.transpose(bank[:, i * P : (i + 1) * P], decayed[:, block], identity[:])
-            turned_banks.append(bank)
+                nc.tensor.transpose(turned_bank[:, i * P : (i + 1) * P], decayed[:, block], identity[:])
+            turned_banks.append(turned_bank)
         base_turned = sb.tile([P, HALF], F32)
         base_banks = []
-        for j in range(2):
-            bank = pair_psum.tile([P, BANK], F32, name="base_bank")
+        for j in range(TURNED_QUARTERS):
+            base_bank = pair_psum.tile([P, BANK], F32, name="base_bank")
             for i in range(BLOCKS):
                 block = slice(j * BANK + i * P, j * BANK + (i + 1) * P)
                 nc.scalar.activation(
                     base_turned[:, block],
                     turned_banks[j][:, i * P : (i + 1) * P],
                     ACT.Identity,
-                    bias=debit_cols[(2 + j) * BLOCKS + i],
+                    bias=debit_cols[(VECTOR_QUARTERS + j) * BLOCKS + i],
                 )
             for i in range(BLOCKS):
                 block = slice(j * BANK + i * P, j * BANK + (i + 1) * P)
-                nc.tensor.transpose(bank[:, i * P : (i + 1) * P], base_turned[:, block], identity[:])
-            base_banks.append(bank)
+                nc.tensor.transpose(base_bank[:, i * P : (i + 1) * P], base_turned[:, block], identity[:])
+            base_banks.append(base_bank)
 
         updated = sb.tile([P, T], F32)
         nc.vector.scalar_tensor_tensor(
             updated[:, :HALF], placed[:, :HALF], row_factor[:], base[:], ALU.mult, ALU.add
         )
-        for j in range(2):
+        for j in range(TURNED_QUARTERS):
             cols = slice(HALF + j * BANK, HALF + (j + 1) * BANK)
             nc.vector.scalar_tensor_tensor(
                 updated[:, cols], placed[:, cols], row_factor[:], base_banks[j][:], ALU.mult, ALU.add

@@ -10,12 +10,11 @@ QUADRANT = 32
 SCALE_ROWS = 4
 BANK = 512
 BLOCKS = BANK // P
-HALF = T // 2
-VECTOR_QUARTERS = HALF // BANK
-TURNED_QUARTERS = (T - HALF) // BANK
+QUARTERS = T // BANK
+BANK_BYTES = 4 * BANK
 CREDIT_ROWS = T // P
 FIRST_CREDIT_ROW = P - CREDIT_ROWS
-WEIGHT_SCALE = 2.0 * 512.0
+WEIGHT_SCALE = 512.0
 
 F32 = mybir.dt.float32
 BF16 = mybir.dt.bfloat16
@@ -35,25 +34,22 @@ def tile_attend_evictscores_kernel(tc, query, keys_words, keys_scales, mass, dec
     nc = tc.nc
     with ExitStack() as ctx:
         sb = ctx.enter_context(tc.tile_pool(name="sb", bufs=1))
-        score_psum = ctx.enter_context(tc.psum_pool(name="score_psum", bufs=1))
-        pair_psum = ctx.enter_context(tc.psum_pool(name="pair_psum", bufs=2))
+        held = ctx.enter_context(tc.tile_pool(name="held", bufs=1))
+        ps = ctx.enter_context(tc.psum_pool(name="ps", bufs=1))
 
         slots = sb.tile([P, I // LIST_ROWS], U16)
         nc.sync.dma_start(slots[:], offs)
-
         credit_rows = sb.tile([P, P], F32)
         nc.scalar.dma_start(credit_rows[FIRST_CREDIT_ROW:, :], credit.rearrange("o (c p) -> (o c) p", p=P))
         nc.gpsimd.memset(credit_rows[:FIRST_CREDIT_ROW, :], 0.0)
-        minus_two = sb.tile([P, 1], F32, align_bytes=64, tag="query_bf")
-        nc.gpsimd.memset(minus_two[:], -2.0)
-
-        candidates = sb.tile([P, J // LIST_ROWS], U16)
-        nc.sync.dma_start(candidates[:], offs2)
+        minus_one = sb.tile([P, 1], F32, align_bytes=64, tag="query_bf")
+        nc.gpsimd.memset(minus_one[:], -1.0)
         word_pool = sb.tile([P, T], U16, align_bytes=64, tag="word_pool")
         nc.sync.dma_start(word_pool[:].bitcast(I32), keys_words[0].bitcast(I32))
+        candidates = sb.tile([P, J // LIST_ROWS], U16)
+        nc.sync.dma_start(candidates[:], offs2)
         query_raw = sb.tile([P, PACK, Q], F32)
         nc.sync.dma_start(query_raw[:], query.rearrange("(p j) q -> p j q", j=PACK))
-
         scale_pool = sb.tile([P, T], U8, align_bytes=64)
         nc.vector.memset(scale_pool[:].bitcast(I32), 0)
         for quad in range(P // QUADRANT):
@@ -61,53 +57,42 @@ def tile_attend_evictscores_kernel(tc, query, keys_words, keys_scales, mass, dec
                 scale_pool[QUADRANT * quad : QUADRANT * quad + SCALE_ROWS, :].bitcast(I32),
                 keys_scales[0, SCALE_ROWS * quad : SCALE_ROWS * (quad + 1), :].bitcast(I32),
             )
-
-        ones = sb.tile([P, P], F32, tag="late")
+        ones = held.tile([P, P], F32, offset=0)
         nc.vector.memset(ones[:], 1.0)
         identity = sb.tile([P, P], F32)
         nc.gpsimd.affine_select(
-            out=identity[:],
-            in_=ones[:],
-            pattern=[[-1, P]],
-            compare_op=ALU.is_equal,
-            fill=0.0,
-            base=0,
+            out=identity[:], in_=ones[:], pattern=[[-1, P]], compare_op=ALU.is_equal, fill=0.0, base=0,
             channel_multiplier=1,
         )
+        twos = sb.tile([P, J // 2], F32)
+        nc.gpsimd.memset(twos[:], 2.0)
         placed = sb.tile([P, T], F32)
         nc.vector.memset(placed[:], 0.0)
 
-        late = sb.tile([P, T + 1], F32, tag="late")
+        late = held.tile([P, T + 1], F32, offset=0)
         decay = late[:, T : T + 1]
+        nc.sync.dma_start(late[:, : T // 2], mass[:, : T // 2])
         nc.sync.dma_start(decay, dec)
-        nc.sync.dma_start(late[:, :HALF], mass[:, :HALF])
-        nc.sync.dma_start(late[:, HALF:T], mass[:, HALF:])
+        nc.sync.dma_start(late[:, T // 2 : T], mass[:, T // 2 :])
+        masses = [late[:, k * BANK : (k + 1) * BANK] for k in range(QUARTERS)]
 
-        credit_turned = score_psum.tile([P, P], F32)
+        credit_turned = ps.tile([P, P], F32, offset=7 * BANK_BYTES)
         nc.tensor.transpose(credit_turned[:], credit_rows[:], identity[:])
         debit_first = sb.tile([P, BLOCKS], F32, align_bytes=64, tag="debit_first")
-        nc.scalar.mul(debit_first[:], credit_turned[:, FIRST_CREDIT_ROW : FIRST_CREDIT_ROW + BLOCKS], minus_two[:])
+        nc.scalar.mul(debit_first[:], credit_turned[:, FIRST_CREDIT_ROW : FIRST_CREDIT_ROW + BLOCKS], minus_one[:])
         debit_rest = sb.tile([P, CREDIT_ROWS - BLOCKS], F32)
-        nc.scalar.mul(debit_rest[:], credit_turned[:, FIRST_CREDIT_ROW + BLOCKS :], minus_two[:])
-        debit_cols = [debit_first[:, c : c + 1] for c in range(BLOCKS)]
-        debit_cols.extend(debit_rest[:, c : c + 1] for c in range(CREDIT_ROWS - BLOCKS))
-
-        def spread_debit(quarter):
-            debit_bank = pair_psum.tile([P, BANK], F32, name="debit_bank")
-            for i in range(BLOCKS):
-                column = debit_cols[quarter * BLOCKS + i]
-                nc.tensor.transpose(debit_bank[:, i * P : (i + 1) * P], column.to_broadcast([P, P]), identity[:])
-            return debit_bank
-
-        first_debit_bank = spread_debit(0)
-
-        key_words = sb.tile([P, I], U16, align_bytes=64)
-        nc.vector.tensor_copy(key_words[:], word_pool[:].indirect(slots[:]))
+        nc.scalar.mul(debit_rest[:], credit_turned[:, FIRST_CREDIT_ROW + BLOCKS :], minus_one[:])
+        debit_bank = ps.tile([P, BANK], F32, offset=4 * BANK_BYTES)
+        for i in range(BLOCKS):
+            nc.tensor.transpose(debit_bank[:, i * P : (i + 1) * P], debit_first[:, i : i + 1].to_broadcast([P, P]), identity[:])
 
         half_list = I // 2 // LIST_ROWS
-        key_scales_lo = sb.tile([P, I // 2], U8, align_bytes=64)
-        nc.vector.tensor_copy(key_scales_lo[:], scale_pool[:].indirect(slots[:, :half_list]))
-
+        H = I // 2
+        lists = [slots[:, :half_list], slots[:, half_list:]]
+        key_words = sb.tile([P, I], U16, align_bytes=64)
+        nc.vector.tensor_copy(key_words[:], word_pool[:].indirect(slots[:]))
+        key_scales_lo = sb.tile([P, H], U8, align_bytes=64)
+        nc.vector.tensor_copy(key_scales_lo[:], scale_pool[:].indirect(lists[0]))
         query_bf = sb.tile([P, Q, PACK], BF16, align_bytes=64, tag="query_bf")
         nc.scalar.copy(
             query_bf[:].rearrange("p (c i) j -> p c j i", i=PACK),
@@ -120,86 +105,74 @@ def tile_attend_evictscores_kernel(tc, query, keys_words, keys_scales, mass, dec
             scales=query_scales[:],
             in_=query_bf[:].rearrange("p q j -> p (q j)"),
         )
-
-        key_scales_hi = sb.tile([P, I // 2], U8, align_bytes=64, tag="query_bf")
-        nc.vector.tensor_copy(key_scales_hi[:], scale_pool[:].indirect(slots[:, half_list:]))
-
-        decay2_first = sb.tile([P, 1], F32, tag="decay2_first")
-        nc.scalar.mul(decay2_first[:], decay, 2.0)
-        decay2 = sb.tile([P, 1], F32)
-        nc.scalar.mul(decay2[:], decay, 2.0)
-        base = sb.tile([P, HALF], F32)
-        minus_one = base[:, HALF - 1 : HALF]
-        nc.gpsimd.memset(minus_one, -1.0)
-
-        def base_on_vector(quarter, debit_bank, doubled_decay):
-            cols = slice(quarter * BANK, (quarter + 1) * BANK)
-            nc.vector.scalar_tensor_tensor(
-                base[:, cols], late[:, cols], doubled_decay[:], debit_bank[:], ALU.mult, ALU.add
-            )
-
-        scores = score_psum.tile([P, I], F32)
+        key_scales_hi = sb.tile([P, H], U8, align_bytes=64, tag="query_bf")
+        nc.vector.tensor_copy(key_scales_hi[:], scale_pool[:].indirect(lists[1]))
+        score_banks = []
         for half, key_scales in enumerate((key_scales_lo, key_scales_hi)):
-            half_slots = slice(half * (I // 2), (half + 1) * (I // 2))
+            score_pair = ps.tile([P, 2 * BANK], F32, offset=2 * half * BANK_BYTES, name="scores%d" % half)
+            scores = score_pair[:, :H]
             nc.tensor.matmul_mx(
-                out=scores[:, half_slots],
+                out=scores,
                 lhsT=query_codes[:].bitcast(FP8X4),
                 lhsT_scale=query_scales[:],
-                rhs=key_words[:, half_slots].bitcast(FP4X4),
+                rhs=key_words[:, half * H : (half + 1) * H].bitcast(FP4X4),
                 rhs_scale=key_scales[:],
                 start=True,
                 stop=True,
             )
-        base_on_vector(0, first_debit_bank, decay2_first)
-        neg_max = sb.tile([P, 1], F32, tag="decay2_first")
+            score_banks.append(scores)
         neg_scores = sb.tile([P, I], F32)
-        nc.vector.tensor_scalar(neg_scores[:], scores[:], minus_one, None, ALU.mult, ALU.min, accum_out=neg_max[:])
-        weights = sb.tile([P, I], F32)
+        neg_max_lo = sb.tile([P, 1], F32, tag="base0")
+        nc.vector.tensor_scalar(neg_scores[:, :H], score_banks[0], -1.0, None, ALU.mult, ALU.min, accum_out=neg_max_lo[:])
+        neg_max = sb.tile([P, 1], F32, tag="decayed_late")
+        nc.vector.tensor_scalar(neg_scores[:, H:], score_banks[1], -1.0, neg_max_lo[:], ALU.mult, ALU.min, accum_out=neg_max[:])
+
+        base0 = sb.tile([P, BANK], F32, tag="base0")
+        nc.vector.scalar_tensor_tensor(base0[:], masses[0], decay, debit_bank[:], ALU.mult, ALU.add)
+        decay_early = sb.tile([P, 1], F32, tag="weights")
+        nc.scalar.copy(decay_early[:], decay)
+        decayed1 = sb.tile([P, BANK], F32)
+        nc.scalar.mul(decayed1[:], masses[1], decay_early[:])
+        decayed = [decayed1[:]]
+
+        weights = sb.tile([P, I], F32, tag="weights")
         row_sum = sb.tile([P, 1], F32)
         nc.scalar.activation(weights[:], neg_scores[:], ACT.Exp, bias=neg_max[:], scale=-1.0, accum_out=row_sum[:])
-        base_on_vector(1, spread_debit(1), decay2)
         nc.vector.tensor_copy(placed[:].indirect(slots[:]), weights[:])
         row_sum_scaled = sb.tile([P, 1], F32)
         nc.scalar.mul(row_sum_scaled[:], row_sum[:], 1.0 / WEIGHT_SCALE)
         row_factor = sb.tile([P, 1], F32)
         nc.vector.reciprocal(row_factor[:], row_sum_scaled[:])
 
-        decayed = sb.tile([P, HALF], F32, tag="decay2_first")
-        turned_banks = []
-        for j in range(TURNED_QUARTERS):
-            cols = slice(j * BANK, (j + 1) * BANK)
-            nc.scalar.mul(decayed[:, cols], late[:, HALF + j * BANK : HALF + (j + 1) * BANK], decay2[:])
-            turned_bank = pair_psum.tile([P, BANK], F32, name="turned_bank")
+        decayed_late = sb.tile([P, 2, BANK], F32, tag="decayed_late")
+        for k in range(2):
+            nc.scalar.mul(decayed_late[:, k, :], masses[2 + k], decay)
+            decayed.append(decayed_late[:, k, :])
+        bases = [base0]
+        for j in range(QUARTERS - 1):
+            turned_bank = ps.tile([P, BANK], F32, offset=j * BANK_BYTES, name="turned%d" % j)
             for i in range(BLOCKS):
-                block = slice(j * BANK + i * P, j * BANK + (i + 1) * P)
-                nc.tensor.transpose(turned_bank[:, i * P : (i + 1) * P], decayed[:, block], identity[:])
-            turned_banks.append(turned_bank)
-        base_turned = sb.tile([P, HALF], F32)
-        base_banks = []
-        for j in range(TURNED_QUARTERS):
-            base_bank = pair_psum.tile([P, BANK], F32, name="base_bank")
+                nc.tensor.transpose(turned_bank[:, i * P : (i + 1) * P], decayed[j][:, i * P : (i + 1) * P], identity[:])
+            base_turned = sb.tile([P, BANK], F32, name="base_turned%d" % j)
             for i in range(BLOCKS):
-                block = slice(j * BANK + i * P, j * BANK + (i + 1) * P)
+                c = j * BLOCKS + i
                 nc.scalar.activation(
-                    base_turned[:, block],
-                    turned_banks[j][:, i * P : (i + 1) * P],
-                    ACT.Identity,
-                    bias=debit_cols[(VECTOR_QUARTERS + j) * BLOCKS + i],
+                    base_turned[:, i * P : (i + 1) * P], turned_bank[:, i * P : (i + 1) * P], ACT.Identity,
+                    bias=debit_rest[:, c : c + 1],
                 )
+            base_bank = ps.tile([P, BANK], F32, offset=(5 + j) * BANK_BYTES, name="base_bank%d" % j)
             for i in range(BLOCKS):
-                block = slice(j * BANK + i * P, j * BANK + (i + 1) * P)
-                nc.tensor.transpose(base_bank[:, i * P : (i + 1) * P], base_turned[:, block], identity[:])
-            base_banks.append(base_bank)
+                nc.tensor.transpose(base_bank[:, i * P : (i + 1) * P], base_turned[:, i * P : (i + 1) * P], identity[:])
+            bases.append(base_bank)
 
         updated = sb.tile([P, T], F32)
-        nc.vector.scalar_tensor_tensor(
-            updated[:, :HALF], placed[:, :HALF], row_factor[:], base[:], ALU.mult, ALU.add
-        )
-        for j in range(TURNED_QUARTERS):
-            cols = slice(HALF + j * BANK, HALF + (j + 1) * BANK)
-            nc.vector.scalar_tensor_tensor(
-                updated[:, cols], placed[:, cols], row_factor[:], base_banks[j][:], ALU.mult, ALU.add
-            )
-        picked = sb.tile([P, J], F32)
-        nc.vector.tensor_copy(picked[:], updated[:].indirect(candidates[:]))
-        nc.sync.dma_start(out, picked[:])
+        for k in range(QUARTERS):
+            cols = slice(k * BANK, (k + 1) * BANK)
+            nc.vector.scalar_tensor_tensor(updated[:, cols], placed[:, cols], row_factor[:], bases[k][:], ALU.mult, ALU.add)
+        half_cand = J // 2 // LIST_ROWS
+        picked_lo = sb.tile([P, J // 2], F32)
+        nc.vector.tensor_tensor(picked_lo[:], updated[:].indirect(candidates[:, :half_cand]), twos[:], ALU.mult)
+        nc.sync.dma_start(out[:, : J // 2], picked_lo[:])
+        picked_hi = sb.tile([P, J // 2], F32)
+        nc.scalar.activation(picked_hi[:], updated[:].indirect(candidates[:, half_cand:]), ACT.Copy, scale=2.0)
+        nc.scalar.dma_start(out[:, J // 2 :], picked_hi[:])

@@ -52,10 +52,9 @@ def tile_attend_evictscores_kernel(tc, query, keys_words, keys_scales, mass, dec
         nc.sync.dma_start(query_raw[:], query.rearrange("(p j) q -> p j q", j=PACK))
         scale_pool = sb.tile([P, T], U8, align_bytes=64)
         nc.vector.memset(scale_pool[:].bitcast(I32), 0)
-        for quad in range(P // QUADRANT):
+        for row in range(SCALE_ROWS):
             nc.sync.dma_start(
-                scale_pool[QUADRANT * quad : QUADRANT * quad + SCALE_ROWS, :].bitcast(I32),
-                keys_scales[0, SCALE_ROWS * quad : SCALE_ROWS * (quad + 1), :].bitcast(I32),
+                scale_pool[row:P:QUADRANT, :].bitcast(I32), keys_scales[0, row::SCALE_ROWS, :].bitcast(I32)
             )
         ones = held.tile([P, P], F32, offset=0)
         nc.vector.memset(ones[:], 1.0)

@@ -15,6 +15,7 @@ BANK_BYTES = 4 * BANK
 CREDIT_ROWS = T // P
 FIRST_CREDIT_ROW = P - CREDIT_ROWS
 WEIGHT_SCALE = 512.0
+GPSIMD_COLS = 384
 
 F32 = mybir.dt.float32
 BF16 = mybir.dt.bfloat16
@@ -126,13 +127,15 @@ def tile_attend_evictscores_kernel(tc, query, keys_words, keys_scales, mass, dec
         neg_max = sb.tile([P, 1], F32, tag="decayed_late")
         nc.vector.tensor_scalar(neg_scores[:, H:], score_banks[1], -1.0, neg_max_lo[:], ALU.mult, ALU.min, accum_out=neg_max[:])
 
-        base0 = sb.tile([P, BANK], F32, tag="base0")
-        nc.vector.scalar_tensor_tensor(base0[:], masses[0], decay, debit_bank[:], ALU.mult, ALU.add)
+        gap_work = sb.tile([P, 2, BANK], F32, tag="base0")
+        base0 = gap_work[:, 0, :]
+        nc.vector.scalar_tensor_tensor(base0, masses[0], decay, debit_bank[:], ALU.mult, ALU.add)
+        nc.vector.tensor_scalar(gap_work[:, 1, :], masses[2], decay, None, ALU.mult)
         decay_early = sb.tile([P, 1], F32, tag="weights")
         nc.scalar.copy(decay_early[:], decay)
         decayed1 = sb.tile([P, BANK], F32)
         nc.scalar.mul(decayed1[:], masses[1], decay_early[:])
-        decayed = [decayed1[:]]
+        decayed = [decayed1[:], gap_work[:, 1, :]]
 
         weights = sb.tile([P, I], F32, tag="weights")
         row_sum = sb.tile([P, 1], F32)
@@ -143,10 +146,9 @@ def tile_attend_evictscores_kernel(tc, query, keys_words, keys_scales, mass, dec
         row_factor = sb.tile([P, 1], F32)
         nc.vector.reciprocal(row_factor[:], row_sum_scaled[:])
 
-        decayed_late = sb.tile([P, 2, BANK], F32, tag="decayed_late")
-        for k in range(2):
-            nc.scalar.mul(decayed_late[:, k, :], masses[2 + k], decay)
-            decayed.append(decayed_late[:, k, :])
+        decayed_late = sb.tile([P, BANK], F32, tag="decayed_late")
+        nc.scalar.mul(decayed_late[:], masses[3], decay)
+        decayed.append(decayed_late[:])
         bases = [base0]
         for j in range(QUARTERS - 1):
             turned_bank = ps.tile([P, BANK], F32, offset=j * BANK_BYTES, name="turned%d" % j)
@@ -165,9 +167,15 @@ def tile_attend_evictscores_kernel(tc, query, keys_words, keys_scales, mass, dec
             bases.append(base_bank)
 
         updated = sb.tile([P, T], F32)
-        for k in range(QUARTERS):
+        shared = slice(0, GPSIMD_COLS)
+        placed_scaled = sb.tile([P, GPSIMD_COLS], F32)
+        nc.gpsimd.tensor_scalar(placed_scaled[:], placed[:, shared], row_factor[:], 0.0, ALU.mult, ALU.add)
+        nc.gpsimd.tensor_tensor(updated[:, shared], placed_scaled[:], base0[:, shared], ALU.add)
+        for k in range(1, QUARTERS):
             cols = slice(k * BANK, (k + 1) * BANK)
             nc.vector.scalar_tensor_tensor(updated[:, cols], placed[:, cols], row_factor[:], bases[k][:], ALU.mult, ALU.add)
+        cols = slice(GPSIMD_COLS, BANK)
+        nc.vector.scalar_tensor_tensor(updated[:, cols], placed[:, cols], row_factor[:], base0[:, cols], ALU.mult, ALU.add)
         half_cand = J // 2 // LIST_ROWS
         picked_lo = sb.tile([P, J // 2], F32)
         nc.vector.tensor_tensor(picked_lo[:], updated[:].indirect(candidates[:, :half_cand]), twos[:], ALU.mult)

@@ -71,9 +71,9 @@ def tile_attend_evictscores_kernel(tc, query, keys_words, keys_scales, mass, dec
 
         late = held.tile([P, T + 1], F32, offset=0)
         decay = late[:, T : T + 1]
-        nc.sync.dma_start(late[:, : T // 2], mass[:, : T // 2])
         nc.sync.dma_start(decay, dec)
-        nc.sync.dma_start(late[:, T // 2 : T], mass[:, T // 2 :])
+        for k in (1, 0, 2, 3):
+            nc.sync.dma_start(late[:, k * BANK : (k + 1) * BANK], mass[:, k * BANK : (k + 1) * BANK])
         masses = [late[:, k * BANK : (k + 1) * BANK] for k in range(QUARTERS)]
 
         credit_turned = ps.tile([P, P], F32, offset=7 * BANK_BYTES)

@@ -51,7 +51,7 @@ def tile_attend_evictscores_kernel(tc, query, keys_words, keys_scales, mass, dec
         nc.sync.dma_start(candidates[:], offs2)
         query_raw = sb.tile([P, PACK, Q], F32)
         nc.sync.dma_start(query_raw[:], query.rearrange("(p j) q -> p j q", j=PACK))
-        scale_pool = sb.tile([P, T], U8, align_bytes=64)
+        scale_pool = sb.tile([P, T], U8, align_bytes=64, tag="scale_pool")
         nc.vector.memset(scale_pool[:].bitcast(I32), 0)
         for row in range(SCALE_ROWS):
             nc.sync.dma_start(
@@ -131,13 +131,11 @@ def tile_attend_evictscores_kernel(tc, query, keys_words, keys_scales, mass, dec
         base0 = gap_work[:, 0, :]
         nc.vector.scalar_tensor_tensor(base0, masses[0], decay, debit_bank[:], ALU.mult, ALU.add)
         nc.vector.tensor_scalar(gap_work[:, 1, :], masses[2], decay, None, ALU.mult)
-        decay_early = sb.tile([P, 1], F32, tag="weights")
-        nc.scalar.copy(decay_early[:], decay)
-        decayed1 = sb.tile([P, BANK], F32)
-        nc.scalar.mul(decayed1[:], masses[1], decay_early[:])
+        decayed1 = sb.tile([P, BANK], F32, align_bytes=64, tag="scale_pool")
+        nc.gpsimd.tensor_scalar(decayed1[:], masses[1], decay, 0.0, ALU.mult, ALU.add)
         decayed = [decayed1[:], gap_work[:, 1, :]]
 
-        weights = sb.tile([P, I], F32, tag="weights")
+        weights = sb.tile([P, I], F32)
         row_sum = sb.tile([P, 1], F32)
         nc.scalar.activation(weights[:], neg_scores[:], ACT.Exp, bias=neg_max[:], scale=-1.0, accum_out=row_sum[:])
         nc.vector.tensor_copy(placed[:].indirect(slots[:]), weights[:])

@@ -127,13 +127,11 @@ def tile_attend_evictscores_kernel(tc, query, keys_words, keys_scales, mass, dec
         neg_max = sb.tile([P, 1], F32, tag="decayed_late")
         nc.vector.tensor_scalar(neg_scores[:, H:], score_banks[1], -1.0, neg_max_lo[:], ALU.mult, ALU.min, accum_out=neg_max[:])
 
-        gap_work = sb.tile([P, 2, BANK], F32, tag="base0")
-        base0 = gap_work[:, 0, :]
-        nc.vector.scalar_tensor_tensor(base0, masses[0], decay, debit_bank[:], ALU.mult, ALU.add)
-        nc.vector.tensor_scalar(gap_work[:, 1, :], masses[2], decay, None, ALU.mult)
+        base0 = sb.tile([P, BANK], F32, tag="base0")
+        nc.vector.scalar_tensor_tensor(base0[:], masses[0], decay, debit_bank[:], ALU.mult, ALU.add)
         decayed1 = sb.tile([P, BANK], F32, align_bytes=64, tag="scale_pool")
         nc.gpsimd.tensor_scalar(decayed1[:], masses[1], decay, 0.0, ALU.mult, ALU.add)
-        decayed = [decayed1[:], gap_work[:, 1, :]]
+        decayed = [decayed1[:]]
 
         weights = sb.tile([P, I], F32)
         row_sum = sb.tile([P, 1], F32)
@@ -144,9 +142,10 @@ def tile_attend_evictscores_kernel(tc, query, keys_words, keys_scales, mass, dec
         row_factor = sb.tile([P, 1], F32)
         nc.vector.reciprocal(row_factor[:], row_sum_scaled[:])
 
-        decayed_late = sb.tile([P, BANK], F32, tag="decayed_late")
-        nc.scalar.mul(decayed_late[:], masses[3], decay)
-        decayed.append(decayed_late[:])
+        decayed_late = sb.tile([P, 2, BANK], F32, tag="decayed_late")
+        for k in range(2):
+            nc.scalar.mul(decayed_late[:, k, :], masses[2 + k], decay)
+            decayed.append(decayed_late[:, k, :])
         bases = [base0]
         for j in range(QUARTERS - 1):
             turned_bank = ps.tile([P, BANK], F32, offset=j * BANK_BYTES, name="turned%d" % j)

@@ -15,7 +15,8 @@ BANK_BYTES = 4 * BANK
 CREDIT_ROWS = T // P
 FIRST_CREDIT_ROW = P - CREDIT_ROWS
 WEIGHT_SCALE = 512.0
-GPSIMD_COLS = 384
+GPSIMD_COLS = 448
+FIRST_SHARE = 192
 
 F32 = mybir.dt.float32
 BF16 = mybir.dt.bfloat16
@@ -82,9 +83,20 @@ def tile_attend_evictscores_kernel(tc, query, keys_words, keys_scales, mass, dec
         nc.scalar.mul(debit_first[:], credit_turned[:, FIRST_CREDIT_ROW : FIRST_CREDIT_ROW + BLOCKS], minus_one[:])
         debit_rest = sb.tile([P, CREDIT_ROWS - BLOCKS], F32)
         nc.scalar.mul(debit_rest[:], credit_turned[:, FIRST_CREDIT_ROW + BLOCKS :], minus_one[:])
-        debit_bank = ps.tile([P, BANK], F32, offset=4 * BANK_BYTES)
+        debit_bank = ps.tile([P, BANK], F32, offset=2 * BANK_BYTES)
         for i in range(BLOCKS):
             nc.tensor.transpose(debit_bank[:, i * P : (i + 1) * P], debit_first[:, i : i + 1].to_broadcast([P, P]), identity[:])
+
+        base_banks = []
+        for j in range(QUARTERS - 1):
+            base_bank = ps.tile([P, BANK], F32, offset=(3 + j) * BANK_BYTES, name="base_bank%d" % j)
+            for i in range(BLOCKS):
+                c = j * BLOCKS + i
+                nc.tensor.matmul(
+                    base_bank[:, i * P : (i + 1) * P], debit_rest[:, c : c + 1].to_broadcast([P, P]), identity[:],
+                    is_transpose=True, start=i == 0, stop=False,
+                )
+            base_banks.append(base_bank)
 
         half_list = I // 2 // LIST_ROWS
         H = I // 2
@@ -109,8 +121,8 @@ def tile_attend_evictscores_kernel(tc, query, keys_words, keys_scales, mass, dec
         nc.vector.tensor_copy(key_scales_hi[:], scale_pool[:].indirect(lists[1]))
         score_banks = []
         for half, key_scales in enumerate((key_scales_lo, key_scales_hi)):
-            score_pair = ps.tile([P, 2 * BANK], F32, offset=2 * half * BANK_BYTES, name="scores%d" % half)
-            scores = score_pair[:, :H]
+            score_bank = ps.tile([P, H], F32, offset=half * BANK_BYTES, name="scores%d" % half)
+            scores = score_bank[:]
             nc.tensor.matmul_mx(
                 out=scores,
                 lhsT=query_codes[:].bitcast(FP8X4),
@@ -152,27 +164,24 @@ def tile_attend_evictscores_kernel(tc, query, keys_words, keys_scales, mass, dec
             for i in range(BLOCKS):
                 nc.tensor.transpose(turned_bank[:, i * P : (i + 1) * P], decayed[j][:, i * P : (i + 1) * P], identity[:])
             base_turned = sb.tile([P, BANK], F32, name="base_turned%d" % j)
+            nc.scalar.copy(base_turned[:], turned_bank[:])
             for i in range(BLOCKS):
-                c = j * BLOCKS + i
-                nc.scalar.activation(
-                    base_turned[:, i * P : (i + 1) * P], turned_bank[:, i * P : (i + 1) * P], ACT.Identity,
-                    bias=debit_rest[:, c : c + 1],
+                nc.tensor.matmul(
+                    base_banks[j][:, i * P : (i + 1) * P], base_turned[:, i * P : (i + 1) * P], identity[:],
+                    is_transpose=True, start=False, stop=i == BLOCKS - 1,
                 )
-            base_bank = ps.tile([P, BANK], F32, offset=(5 + j) * BANK_BYTES, name="base_bank%d" % j)
-            for i in range(BLOCKS):
-                nc.tensor.transpose(base_bank[:, i * P : (i + 1) * P], base_turned[:, i * P : (i + 1) * P], identity[:])
-            bases.append(base_bank)
+            bases.append(base_banks[j])
 
         updated = sb.tile([P, T], F32)
-        shared = slice(0, GPSIMD_COLS)
-        placed_scaled = sb.tile([P, GPSIMD_COLS], F32)
-        nc.gpsimd.tensor_scalar(placed_scaled[:], placed[:, shared], row_factor[:], 0.0, ALU.mult, ALU.add)
-        nc.gpsimd.tensor_tensor(updated[:, shared], placed_scaled[:], base0[:, shared], ALU.add)
+        cols = slice(GPSIMD_COLS, BANK)
+        nc.vector.scalar_tensor_tensor(updated[:, cols], placed[:, cols], row_factor[:], base0[:, cols], ALU.mult, ALU.add)
+        placed_scaled = sb.tile([P, GPSIMD_COLS], F32, tag="decayed_late")
+        for shared in (slice(0, FIRST_SHARE), slice(FIRST_SHARE, GPSIMD_COLS)):
+            nc.scalar.mul(placed_scaled[:, shared], placed[:, shared], row_factor[:])
+            nc.gpsimd.tensor_tensor(updated[:, shared], placed_scaled[:, shared], base0[:, shared], ALU.add)
         for k in range(1, QUARTERS):
             cols = slice(k * BANK, (k + 1) * BANK)
             nc.vector.scalar_tensor_tensor(updated[:, cols], placed[:, cols], row_factor[:], bases[k][:], ALU.mult, ALU.add)
-        cols = slice(GPSIMD_COLS, BANK)
-        nc.vector.scalar_tensor_tensor(updated[:, cols], placed[:, cols], row_factor[:], base0[:, cols], ALU.mult, ALU.add)
         half_cand = J // 2 // LIST_ROWS
         picked_lo = sb.tile([P, J // 2], F32)
         nc.vector.tensor_tensor(picked_lo[:], updated[:].indirect(candidates[:, :half_cand]), twos[:], ALU.mult)

@@ -15,8 +15,12 @@ BANK_BYTES = 4 * BANK
 CREDIT_ROWS = T // P
 FIRST_CREDIT_ROW = P - CREDIT_ROWS
 WEIGHT_SCALE = 512.0
-GPSIMD_COLS = 448
-FIRST_SHARE = 192
+GPSIMD_COLS = 384
+FIRST_SLOTS = 64
+LAST_AT = 3 * BANK_BYTES + 32
+EARLY = 5 * P
+DIRECT = slice(EARLY, EARLY + GPSIMD_COLS)
+GROUPS = ((0, 4), (4, 5), (8, 12), (12, 16))
 
 F32 = mybir.dt.float32
 BF16 = mybir.dt.bfloat16
@@ -58,7 +62,7 @@ def tile_attend_evictscores_kernel(tc, query, keys_words, keys_scales, mass, dec
             nc.sync.dma_start(
                 scale_pool[row:P:QUADRANT, :].bitcast(I32), keys_scales[0, row::SCALE_ROWS, :].bitcast(I32)
             )
-        ones = held.tile([P, P], F32, offset=0)
+        ones = held.tile([P, P], F32, offset=LAST_AT - 256)
         nc.vector.memset(ones[:], 1.0)
         identity = sb.tile([P, P], F32)
         nc.gpsimd.affine_select(
@@ -67,39 +71,45 @@ def tile_attend_evictscores_kernel(tc, query, keys_words, keys_scales, mass, dec
         )
         twos = sb.tile([P, J // 2], F32)
         nc.gpsimd.memset(twos[:], 2.0)
+        zeros = sb.tile([P, FIRST_SLOTS], F32)
+        nc.gpsimd.memset(zeros[:], 0.0)
         placed = sb.tile([P, T], F32)
         nc.vector.memset(placed[:], 0.0)
 
-        late = held.tile([P, T + 1], F32, offset=0)
-        decay = late[:, T : T + 1]
+        late = held.tile([P, 3 * BANK + 1], F32, offset=0)
+        mass_last = held.tile([P, BANK], F32, offset=LAST_AT)
+        decay = late[:, 3 * BANK :]
         nc.sync.dma_start(decay, dec)
-        for k in (1, 0, 2, 3):
-            nc.sync.dma_start(late[:, k * BANK : (k + 1) * BANK], mass[:, k * BANK : (k + 1) * BANK])
-        masses = [late[:, k * BANK : (k + 1) * BANK] for k in range(QUARTERS)]
+        for first, last in ((0, EARLY), (EARLY, 2 * BANK), (2 * BANK, 3 * BANK)):
+            nc.sync.dma_start(late[:, first:last], mass[:, first:last])
+        nc.sync.dma_start(mass_last[:], mass[:, 3 * BANK :])
 
         credit_turned = ps.tile([P, P], F32, offset=7 * BANK_BYTES)
         nc.tensor.transpose(credit_turned[:], credit_rows[:], identity[:])
-        debit_first = sb.tile([P, BLOCKS], F32, align_bytes=64, tag="debit_first")
-        nc.scalar.mul(debit_first[:], credit_turned[:, FIRST_CREDIT_ROW : FIRST_CREDIT_ROW + BLOCKS], minus_one[:])
-        debit_rest = sb.tile([P, CREDIT_ROWS - BLOCKS], F32)
-        nc.scalar.mul(debit_rest[:], credit_turned[:, FIRST_CREDIT_ROW + BLOCKS :], minus_one[:])
-        debit_bank = ps.tile([P, BANK], F32, offset=2 * BANK_BYTES)
-        for i in range(BLOCKS):
-            nc.tensor.transpose(debit_bank[:, i * P : (i + 1) * P], debit_first[:, i : i + 1].to_broadcast([P, P]), identity[:])
+        debit = credit_turned[:, FIRST_CREDIT_ROW:]
+        debit_first = sb.tile([P, 2], F32, align_bytes=64, tag="debit_first")
+        nc.scalar.mul(debit_first[:], debit[:, 5:7], minus_one[:])
+        debit_all = sb.tile([P, CREDIT_ROWS], F32)
+        nc.scalar.mul(debit_all[:], debit, minus_one[:])
+        H = I // 2
+        score_lo = ps.tile([P, 3 * BANK], F32, offset=BANK_BYTES)
+        front_hi = ps.tile([P, BANK], F32, offset=0)
+        for i in range(2):
+            nc.tensor.transpose(
+                front_hi[:, H + i * P : H + (i + 1) * P], debit_first[:, i : i + 1].to_broadcast([P, P]), identity[:]
+            )
 
         base_banks = []
-        for j in range(QUARTERS - 1):
-            base_bank = ps.tile([P, BANK], F32, offset=(3 + j) * BANK_BYTES, name="base_bank%d" % j)
-            for i in range(BLOCKS):
-                c = j * BLOCKS + i
+        for j, (first, last) in enumerate(GROUPS):
+            base_bank = ps.tile([P, (last - first) * P], F32, offset=(4, 7, 5, 6)[j] * BANK_BYTES, name="base_bank%d" % j)
+            for c in range(first, last):
                 nc.tensor.matmul(
-                    base_bank[:, i * P : (i + 1) * P], debit_rest[:, c : c + 1].to_broadcast([P, P]), identity[:],
-                    is_transpose=True, start=i == 0, stop=False,
+                    base_bank[:, (c - first) * P : (c - first + 1) * P], debit_all[:, c : c + 1].to_broadcast([P, P]),
+                    identity[:], is_transpose=True, start=c == first, stop=False,
                 )
             base_banks.append(base_bank)
 
         half_list = I // 2 // LIST_ROWS
-        H = I // 2
         lists = [slots[:, :half_list], slots[:, half_list:]]
         key_words = sb.tile([P, I], U16, align_bytes=64)
         nc.vector.tensor_copy(key_words[:], word_pool[:].indirect(slots[:]))
@@ -121,8 +131,7 @@ def tile_attend_evictscores_kernel(tc, query, keys_words, keys_scales, mass, dec
         nc.vector.tensor_copy(key_scales_hi[:], scale_pool[:].indirect(lists[1]))
         score_banks = []
         for half, key_scales in enumerate((key_scales_lo, key_scales_hi)):
-            score_bank = ps.tile([P, H], F32, offset=half * BANK_BYTES, name="scores%d" % half)
-            scores = score_bank[:]
+            scores = (score_lo, front_hi)[half][:, :H]
             nc.tensor.matmul_mx(
                 out=scores,
                 lhsT=query_codes[:].bitcast(FP8X4),
@@ -134,54 +143,61 @@ def tile_attend_evictscores_kernel(tc, query, keys_words, keys_scales, mass, dec
             )
             score_banks.append(scores)
         neg_scores = sb.tile([P, I], F32)
-        neg_max_lo = sb.tile([P, 1], F32, tag="base0")
+        neg_max_lo = sb.tile([P, 1], F32)
         nc.vector.tensor_scalar(neg_scores[:, :H], score_banks[0], -1.0, None, ALU.mult, ALU.min, accum_out=neg_max_lo[:])
         neg_max = sb.tile([P, 1], F32, tag="decayed_late")
         nc.vector.tensor_scalar(neg_scores[:, H:], score_banks[1], -1.0, neg_max_lo[:], ALU.mult, ALU.min, accum_out=neg_max[:])
 
-        base0 = sb.tile([P, BANK], F32, tag="base0")
-        nc.vector.scalar_tensor_tensor(base0[:], masses[0], decay, debit_bank[:], ALU.mult, ALU.add)
-        decayed1 = sb.tile([P, BANK], F32, align_bytes=64, tag="scale_pool")
-        nc.gpsimd.tensor_scalar(decayed1[:], masses[1], decay, 0.0, ALU.mult, ALU.add)
-        decayed = [decayed1[:]]
+        base_direct = sb.tile([P, GPSIMD_COLS], F32)
+        nc.vector.scalar_tensor_tensor(base_direct[:, :H], late[:, EARLY : EARLY + H], decay, front_hi[:, H:], ALU.mult, ALU.add)
+        debit_late = ps.tile([P, P], F32, offset=BANK_BYTES)
+        nc.tensor.transpose(debit_late[:], debit_all[:, 7:8].to_broadcast([P, P]), identity[:])
+        nc.vector.scalar_tensor_tensor(base_direct[:, H:], late[:, EARLY + H : 2 * BANK], decay, debit_late[:], ALU.mult, ALU.add)
+        decayed_early = sb.tile([P, EARLY], F32, align_bytes=64, tag="scale_pool")
+        nc.gpsimd.tensor_scalar(decayed_early[:], late[:, :EARLY], decay, 0.0, ALU.mult, ALU.add)
+        decayed = [decayed_early[:, :BANK], decayed_early[:, BANK:]]
 
         weights = sb.tile([P, I], F32)
-        row_sum = sb.tile([P, 1], F32)
-        nc.scalar.activation(weights[:], neg_scores[:], ACT.Exp, bias=neg_max[:], scale=-1.0, accum_out=row_sum[:])
-        nc.vector.tensor_copy(placed[:].indirect(slots[:]), weights[:])
+        first_cols = FIRST_SLOTS // LIST_ROWS
+        sum_first = sb.tile([P, 1], F32)
+        nc.scalar.activation(
+            weights[:, :FIRST_SLOTS], neg_scores[:, :FIRST_SLOTS], ACT.Exp, bias=neg_max[:], scale=-1.0, accum_out=sum_first[:]
+        )
+        sum_rest = sb.tile([P, 1], F32)
+        nc.scalar.activation(
+            weights[:, FIRST_SLOTS:], neg_scores[:, FIRST_SLOTS:], ACT.Exp, bias=neg_max[:], scale=-1.0, accum_out=sum_rest[:]
+        )
+        nc.vector.tensor_tensor(placed[:].indirect(slots[:, :first_cols]), weights[:, :FIRST_SLOTS], zeros[:], ALU.add)
         row_sum_scaled = sb.tile([P, 1], F32)
-        nc.scalar.mul(row_sum_scaled[:], row_sum[:], 1.0 / WEIGHT_SCALE)
+        nc.vector.tensor_scalar(row_sum_scaled[:], sum_first[:], sum_rest[:], 1.0 / WEIGHT_SCALE, ALU.add, ALU.mult)
+        nc.vector.tensor_copy(placed[:].indirect(slots[:, first_cols:]), weights[:, FIRST_SLOTS:])
         row_factor = sb.tile([P, 1], F32)
         nc.vector.reciprocal(row_factor[:], row_sum_scaled[:])
 
         decayed_late = sb.tile([P, 2, BANK], F32, tag="decayed_late")
-        for k in range(2):
-            nc.scalar.mul(decayed_late[:, k, :], masses[2 + k], decay)
+        for k, source in enumerate((late[:, 2 * BANK : 3 * BANK], mass_last[:])):
+            nc.scalar.mul(decayed_late[:, k, :], source, decay)
             decayed.append(decayed_late[:, k, :])
-        bases = [base0]
-        for j in range(QUARTERS - 1):
-            turned_bank = ps.tile([P, BANK], F32, offset=j * BANK_BYTES, name="turned%d" % j)
-            for i in range(BLOCKS):
+        for j, (first, last) in enumerate(GROUPS):
+            width = (last - first) * P
+            turned_bank = ps.tile([P, width], F32, offset=(2, 3, 0, 1)[j] * BANK_BYTES, name="turned%d" % j)
+            for i in range(last - first):
                 nc.tensor.transpose(turned_bank[:, i * P : (i + 1) * P], decayed[j][:, i * P : (i + 1) * P], identity[:])
-            base_turned = sb.tile([P, BANK], F32, name="base_turned%d" % j)
+            base_turned = held.tile([P, width], F32, name="base_turned%d" % j, offset=LAST_AT + (P * 4, 0, 2 * BANK_BYTES, 3 * BANK_BYTES)[j])
             nc.scalar.copy(base_turned[:], turned_bank[:])
-            for i in range(BLOCKS):
+            for i in range(last - first):
                 nc.tensor.matmul(
                     base_banks[j][:, i * P : (i + 1) * P], base_turned[:, i * P : (i + 1) * P], identity[:],
-                    is_transpose=True, start=False, stop=i == BLOCKS - 1,
+                    is_transpose=True, start=False, stop=i == last - first - 1,
                 )
-            bases.append(base_banks[j])
 
         updated = sb.tile([P, T], F32)
-        cols = slice(GPSIMD_COLS, BANK)
-        nc.vector.scalar_tensor_tensor(updated[:, cols], placed[:, cols], row_factor[:], base0[:, cols], ALU.mult, ALU.add)
-        placed_scaled = sb.tile([P, GPSIMD_COLS], F32, tag="decayed_late")
-        for shared in (slice(0, FIRST_SHARE), slice(FIRST_SHARE, GPSIMD_COLS)):
-            nc.scalar.mul(placed_scaled[:, shared], placed[:, shared], row_factor[:])
-            nc.gpsimd.tensor_tensor(updated[:, shared], placed_scaled[:, shared], base0[:, shared], ALU.add)
-        for k in range(1, QUARTERS):
-            cols = slice(k * BANK, (k + 1) * BANK)
-            nc.vector.scalar_tensor_tensor(updated[:, cols], placed[:, cols], row_factor[:], bases[k][:], ALU.mult, ALU.add)
+        placed_scaled = sb.tile([P, GPSIMD_COLS], F32)
+        nc.gpsimd.tensor_scalar(placed_scaled[:], placed[:, DIRECT], row_factor[:], 0.0, ALU.mult, ALU.add)
+        nc.gpsimd.tensor_tensor(updated[:, DIRECT], placed_scaled[:], base_direct[:], ALU.add)
+        for j, (first, last) in enumerate(GROUPS):
+            cols = slice(first * P, last * P)
+            nc.vector.scalar_tensor_tensor(updated[:, cols], placed[:, cols], row_factor[:], base_banks[j][:], ALU.mult, ALU.add)
         half_cand = J // 2 // LIST_ROWS
         picked_lo = sb.tile([P, J // 2], F32)
         nc.vector.tensor_tensor(picked_lo[:], updated[:].indirect(candidates[:, :half_cand]), twos[:], ALU.mult)

@@ -15,11 +15,12 @@ BANK_BYTES = 4 * BANK
 CREDIT_ROWS = T // P
 FIRST_CREDIT_ROW = P - CREDIT_ROWS
 WEIGHT_SCALE = 512.0
-GPSIMD_COLS = 384
+GPSIMD_COLS = 512
+OWN_SCALED = 224
 FIRST_SLOTS = 64
 LAST_AT = 3 * BANK_BYTES + 32
 EARLY = 5 * P
-DIRECT = slice(EARLY, EARLY + GPSIMD_COLS)
+SHARED = slice(BANK, 2 * BANK)
 GROUPS = ((0, 4), (4, 5), (8, 12), (12, 16))
 
 F32 = mybir.dt.float32
@@ -149,10 +150,10 @@ def tile_attend_evictscores_kernel(tc, query, keys_words, keys_scales, mass, dec
         nc.vector.tensor_scalar(neg_scores[:, H:], score_banks[1], -1.0, neg_max_lo[:], ALU.mult, ALU.min, accum_out=neg_max[:])
 
         base_direct = sb.tile([P, GPSIMD_COLS], F32)
-        nc.vector.scalar_tensor_tensor(base_direct[:, :H], late[:, EARLY : EARLY + H], decay, front_hi[:, H:], ALU.mult, ALU.add)
+        nc.vector.scalar_tensor_tensor(base_direct[:, P : P + H], late[:, EARLY : EARLY + H], decay, front_hi[:, H:], ALU.mult, ALU.add)
         debit_late = ps.tile([P, P], F32, offset=BANK_BYTES)
         nc.tensor.transpose(debit_late[:], debit_all[:, 7:8].to_broadcast([P, P]), identity[:])
-        nc.vector.scalar_tensor_tensor(base_direct[:, H:], late[:, EARLY + H : 2 * BANK], decay, debit_late[:], ALU.mult, ALU.add)
+        nc.vector.scalar_tensor_tensor(base_direct[:, P + H :], late[:, EARLY + H : 2 * BANK], decay, debit_late[:], ALU.mult, ALU.add)
         decayed_early = sb.tile([P, EARLY], F32, align_bytes=64, tag="scale_pool")
         nc.gpsimd.tensor_scalar(decayed_early[:], late[:, :EARLY], decay, 0.0, ALU.mult, ALU.add)
         decayed = [decayed_early[:, :BANK], decayed_early[:, BANK:]]
@@ -178,7 +179,8 @@ def tile_attend_evictscores_kernel(tc, query, keys_words, keys_scales, mass, dec
         for k, source in enumerate((late[:, 2 * BANK : 3 * BANK], mass_last[:])):
             nc.scalar.mul(decayed_late[:, k, :], source, decay)
             decayed.append(decayed_late[:, k, :])
-        for j, (first, last) in enumerate(GROUPS):
+        for j in (1, 0, 2, 3):
+            first, last = GROUPS[j]
             width = (last - first) * P
             turned_bank = ps.tile([P, width], F32, offset=(2, 3, 0, 1)[j] * BANK_BYTES, name="turned%d" % j)
             for i in range(last - first):
@@ -191,12 +193,17 @@ def tile_attend_evictscores_kernel(tc, query, keys_words, keys_scales, mass, dec
                     is_transpose=True, start=False, stop=i == last - first - 1,
                 )
 
+        nc.scalar.copy(base_direct[:, :P], base_banks[1][:])
+
         updated = sb.tile([P, T], F32)
-        placed_scaled = sb.tile([P, GPSIMD_COLS], F32)
-        nc.gpsimd.tensor_scalar(placed_scaled[:], placed[:, DIRECT], row_factor[:], 0.0, ALU.mult, ALU.add)
-        nc.gpsimd.tensor_tensor(updated[:, DIRECT], placed_scaled[:], base_direct[:], ALU.add)
-        for j, (first, last) in enumerate(GROUPS):
-            cols = slice(first * P, last * P)
+        placed_scaled = sb.tile([P, GPSIMD_COLS], F32, tag="decayed_late")
+        nc.gpsimd.tensor_scalar(
+            placed_scaled[:, :OWN_SCALED], placed[:, BANK : BANK + OWN_SCALED], row_factor[:], 0.0, ALU.mult, ALU.add
+        )
+        nc.scalar.mul(placed_scaled[:, OWN_SCALED:], placed[:, BANK + OWN_SCALED : 2 * BANK], row_factor[:])
+        nc.gpsimd.tensor_tensor(updated[:, SHARED], placed_scaled[:], base_direct[:], ALU.add)
+        for j in (0, 2, 3):
+            cols = slice(GROUPS[j][0] * P, GROUPS[j][1] * P)
             nc.vector.scalar_tensor_tensor(updated[:, cols], placed[:, cols], row_factor[:], base_banks[j][:], ALU.mult, ALU.add)
         half_cand = J // 2 // LIST_ROWS
         picked_lo = sb.tile([P, J // 2], F32)

@@ -18,10 +18,9 @@ WEIGHT_SCALE = 512.0
 GPSIMD_COLS = 512
 OWN_SCALED = 224
 FIRST_SLOTS = 64
-LAST_AT = 3 * BANK_BYTES + 32
-EARLY = 5 * P
-SHARED = slice(BANK, 2 * BANK)
-GROUPS = ((0, 4), (4, 5), (8, 12), (12, 16))
+LAST_AT = 12 * P * 4 + 32
+EARLY = T - 5 * P
+TURNED = (3, 1, 2)
 
 F32 = mybir.dt.float32
 BF16 = mybir.dt.bfloat16
@@ -77,44 +76,46 @@ def tile_attend_evictscores_kernel(tc, query, keys_words, keys_scales, mass, dec
         placed = sb.tile([P, T], F32)
         nc.vector.memset(placed[:], 0.0)
 
-        late = held.tile([P, 3 * BANK + 1], F32, offset=0)
+        late = held.tile([P, 12 * P + 1], F32, offset=0)
         mass_last = held.tile([P, BANK], F32, offset=LAST_AT)
-        decay = late[:, 3 * BANK :]
+        mass_early = late[:, 7 * P : 12 * P]
+        decay = late[:, 12 * P :]
         nc.sync.dma_start(decay, dec)
-        for first, last in ((0, EARLY), (EARLY, 2 * BANK), (2 * BANK, 3 * BANK)):
-            nc.sync.dma_start(late[:, first:last], mass[:, first:last])
-        nc.sync.dma_start(mass_last[:], mass[:, 3 * BANK :])
+        nc.sync.dma_start(mass_early, mass[:, EARLY:])
+        nc.sync.dma_start(late[:, : 3 * P], mass[:, : 3 * P])
+        nc.sync.dma_start(late[:, 3 * P : 7 * P], mass[:, 3 * P : 7 * P])
+        nc.sync.dma_start(mass_last[:], mass[:, 7 * P : EARLY])
 
-        credit_turned = ps.tile([P, P], F32, offset=7 * BANK_BYTES)
-        nc.tensor.transpose(credit_turned[:], credit_rows[:], identity[:])
+        credit_banks = ps.tile([P, 2 * BANK], F32, offset=6 * BANK_BYTES)
+        credit_turned = credit_banks[:, :P]
+        nc.tensor.transpose(credit_turned, credit_rows[:], identity[:])
         debit = credit_turned[:, FIRST_CREDIT_ROW:]
-        debit_first = sb.tile([P, 2], F32, align_bytes=64, tag="debit_first")
-        nc.scalar.mul(debit_first[:], debit[:, 5:7], minus_one[:])
-        debit_all = sb.tile([P, CREDIT_ROWS], F32)
-        nc.scalar.mul(debit_all[:], debit, minus_one[:])
+        debit_first = sb.tile([P, 3], F32, align_bytes=64, tag="debit_first")
+        nc.scalar.mul(debit_first[:], debit[:, 1:BLOCKS], minus_one[:])
+        debit_rest = sb.tile([P, CREDIT_ROWS - BLOCKS], F32)
+        nc.scalar.mul(debit_rest[:], debit[:, BLOCKS:], minus_one[:])
         H = I // 2
-        score_lo = ps.tile([P, 3 * BANK], F32, offset=BANK_BYTES)
+        front_lo = ps.tile([P, BANK], F32, offset=BANK_BYTES)
         front_hi = ps.tile([P, BANK], F32, offset=0)
-        for i in range(2):
-            nc.tensor.transpose(
-                front_hi[:, H + i * P : H + (i + 1) * P], debit_first[:, i : i + 1].to_broadcast([P, P]), identity[:]
-            )
+        for i, spread in enumerate((front_hi[:, H : H + P], front_hi[:, H + P :], front_lo[:, H : H + P])):
+            nc.tensor.transpose(spread, debit_first[:, i : i + 1].to_broadcast([P, P]), identity[:])
 
-        base_banks = []
-        for j, (first, last) in enumerate(GROUPS):
-            base_bank = ps.tile([P, (last - first) * P], F32, offset=(4, 7, 5, 6)[j] * BANK_BYTES, name="base_bank%d" % j)
-            for c in range(first, last):
+        base_banks = {}
+        for j, k in enumerate(TURNED):
+            base_bank = ps.tile([P, BANK], F32, offset=(3 + j) * BANK_BYTES, name="base_bank%d" % k)
+            for i in range(BLOCKS):
+                c = (k - 1) * BLOCKS + i
                 nc.tensor.matmul(
-                    base_bank[:, (c - first) * P : (c - first + 1) * P], debit_all[:, c : c + 1].to_broadcast([P, P]),
-                    identity[:], is_transpose=True, start=c == first, stop=False,
+                    base_bank[:, i * P : (i + 1) * P], debit_rest[:, c : c + 1].to_broadcast([P, P]),
+                    identity[:], is_transpose=True, start=i == 0, stop=False,
                 )
-            base_banks.append(base_bank)
+            base_banks[k] = base_bank
 
         half_list = I // 2 // LIST_ROWS
         lists = [slots[:, :half_list], slots[:, half_list:]]
         key_words = sb.tile([P, I], U16, align_bytes=64)
         nc.vector.tensor_copy(key_words[:], word_pool[:].indirect(slots[:]))
-        key_scales_lo = sb.tile([P, H], U8, align_bytes=64)
+        key_scales_lo = sb.tile([P, H], U8, align_bytes=64, tag="key_scales_lo")
         nc.vector.tensor_copy(key_scales_lo[:], scale_pool[:].indirect(lists[0]))
         query_bf = sb.tile([P, Q, PACK], BF16, align_bytes=64, tag="query_bf")
         nc.scalar.copy(
@@ -132,7 +133,7 @@ def tile_attend_evictscores_kernel(tc, query, keys_words, keys_scales, mass, dec
         nc.vector.tensor_copy(key_scales_hi[:], scale_pool[:].indirect(lists[1]))
         score_banks = []
         for half, key_scales in enumerate((key_scales_lo, key_scales_hi)):
-            scores = (score_lo, front_hi)[half][:, :H]
+            scores = (front_lo, front_hi)[half][:, :H]
             nc.tensor.matmul_mx(
                 out=scores,
                 lhsT=query_codes[:].bitcast(FP8X4),
@@ -150,61 +151,66 @@ def tile_attend_evictscores_kernel(tc, query, keys_words, keys_scales, mass, dec
         nc.vector.tensor_scalar(neg_scores[:, H:], score_banks[1], -1.0, neg_max_lo[:], ALU.mult, ALU.min, accum_out=neg_max[:])
 
         base_direct = sb.tile([P, GPSIMD_COLS], F32)
-        nc.vector.scalar_tensor_tensor(base_direct[:, P : P + H], late[:, EARLY : EARLY + H], decay, front_hi[:, H:], ALU.mult, ALU.add)
-        debit_late = ps.tile([P, P], F32, offset=BANK_BYTES)
-        nc.tensor.transpose(debit_late[:], debit_all[:, 7:8].to_broadcast([P, P]), identity[:])
-        nc.vector.scalar_tensor_tensor(base_direct[:, P + H :], late[:, EARLY + H : 2 * BANK], decay, debit_late[:], ALU.mult, ALU.add)
-        decayed_early = sb.tile([P, EARLY], F32, align_bytes=64, tag="scale_pool")
-        nc.gpsimd.tensor_scalar(decayed_early[:], late[:, :EARLY], decay, 0.0, ALU.mult, ALU.add)
-        decayed = [decayed_early[:, :BANK], decayed_early[:, BANK:]]
+
+        def direct_base(first, last, spread):
+            nc.vector.scalar_tensor_tensor(
+                base_direct[:, first:last], late[:, first:last], decay, spread, ALU.mult, ALU.add
+            )
+
+        direct_base(P, P + H, front_hi[:, H:])
+        debit_last = sb.tile([P, 1], F32, align_bytes=64, tag="key_scales_lo")
+        nc.scalar.mul(debit_last[:], debit[:, :1], -1.0)
+        spread_late = ps.tile([P, P], F32, offset=2 * BANK_BYTES)
+        nc.tensor.transpose(spread_late[:], debit_last[:].to_broadcast([P, P]), identity[:])
+        direct_base(0, P, spread_late[:])
+        decayed_early = sb.tile([P, T - EARLY], F32, align_bytes=64, tag="scale_pool")
+        nc.gpsimd.tensor_scalar(decayed_early[:], mass_early, decay, 0.0, ALU.mult, ALU.add)
 
         weights = sb.tile([P, I], F32)
         first_cols = FIRST_SLOTS // LIST_ROWS
         sum_first = sb.tile([P, 1], F32)
         nc.scalar.activation(
-            weights[:, :FIRST_SLOTS], neg_scores[:, :FIRST_SLOTS], ACT.Exp, bias=neg_max[:], scale=-1.0, accum_out=sum_first[:]
+            weights[:, :FIRST_SLOTS], front_lo[:, :FIRST_SLOTS], ACT.Exp, bias=neg_max[:], accum_out=sum_first[:]
         )
         sum_rest = sb.tile([P, 1], F32)
         nc.scalar.activation(
             weights[:, FIRST_SLOTS:], neg_scores[:, FIRST_SLOTS:], ACT.Exp, bias=neg_max[:], scale=-1.0, accum_out=sum_rest[:]
         )
         nc.vector.tensor_tensor(placed[:].indirect(slots[:, :first_cols]), weights[:, :FIRST_SLOTS], zeros[:], ALU.add)
+        direct_base(H + P, BANK, front_lo[:, H : H + P])
         row_sum_scaled = sb.tile([P, 1], F32)
         nc.vector.tensor_scalar(row_sum_scaled[:], sum_first[:], sum_rest[:], 1.0 / WEIGHT_SCALE, ALU.add, ALU.mult)
         nc.vector.tensor_copy(placed[:].indirect(slots[:, first_cols:]), weights[:, FIRST_SLOTS:])
         row_factor = sb.tile([P, 1], F32)
         nc.vector.reciprocal(row_factor[:], row_sum_scaled[:])
 
-        decayed_late = sb.tile([P, 2, BANK], F32, tag="decayed_late")
-        for k, source in enumerate((late[:, 2 * BANK : 3 * BANK], mass_last[:])):
-            nc.scalar.mul(decayed_late[:, k, :], source, decay)
-            decayed.append(decayed_late[:, k, :])
-        for j in (1, 0, 2, 3):
-            first, last = GROUPS[j]
-            width = (last - first) * P
-            turned_bank = ps.tile([P, width], F32, offset=(2, 3, 0, 1)[j] * BANK_BYTES, name="turned%d" % j)
-            for i in range(last - first):
-                nc.tensor.transpose(turned_bank[:, i * P : (i + 1) * P], decayed[j][:, i * P : (i + 1) * P], identity[:])
-            base_turned = held.tile([P, width], F32, name="base_turned%d" % j, offset=LAST_AT + (P * 4, 0, 2 * BANK_BYTES, 3 * BANK_BYTES)[j])
+        decayed_late = sb.tile([P, EARLY - BANK], F32, tag="decayed_late")
+        nc.scalar.mul(decayed_late[:, : 3 * P], late[:, BANK : 7 * P], decay)
+        nc.scalar.mul(decayed_late[:, 3 * P :], mass_last[:], decay)
+        for j, k in enumerate(TURNED):
+            turned_bank = ps.tile([P, BANK], F32, offset=(6, 0, 7)[j] * BANK_BYTES, name="turned%d" % k)
+            for i in reversed(range(BLOCKS)) if k == 2 else range(BLOCKS):
+                first = k * BANK + i * P
+                source = decayed_early[:, first - EARLY : first - EARLY + P] if first >= EARLY else decayed_late[:, first - BANK : first - BANK + P]
+                nc.tensor.transpose(turned_bank[:, i * P : (i + 1) * P], source, identity[:])
+            base_turned = held.tile([P, BANK], F32, name="base_turned%d" % k, offset=LAST_AT + j * BANK_BYTES)
             nc.scalar.copy(base_turned[:], turned_bank[:])
-            for i in range(last - first):
+            for i in range(BLOCKS):
                 nc.tensor.matmul(
-                    base_banks[j][:, i * P : (i + 1) * P], base_turned[:, i * P : (i + 1) * P], identity[:],
-                    is_transpose=True, start=False, stop=i == last - first - 1,
+                    base_banks[k][:, i * P : (i + 1) * P], base_turned[:, i * P : (i + 1) * P], identity[:],
+                    is_transpose=True, start=False, stop=i == BLOCKS - 1,
                 )
-
-        nc.scalar.copy(base_direct[:, :P], base_banks[1][:])
 
         updated = sb.tile([P, T], F32)
         placed_scaled = sb.tile([P, GPSIMD_COLS], F32, tag="decayed_late")
         nc.gpsimd.tensor_scalar(
-            placed_scaled[:, :OWN_SCALED], placed[:, BANK : BANK + OWN_SCALED], row_factor[:], 0.0, ALU.mult, ALU.add
+            placed_scaled[:, :OWN_SCALED], placed[:, :OWN_SCALED], row_factor[:], 0.0, ALU.mult, ALU.add
         )
-        nc.scalar.mul(placed_scaled[:, OWN_SCALED:], placed[:, BANK + OWN_SCALED : 2 * BANK], row_factor[:])
-        nc.gpsimd.tensor_tensor(updated[:, SHARED], placed_scaled[:], base_direct[:], ALU.add)
-        for j in (0, 2, 3):
-            cols = slice(GROUPS[j][0] * P, GROUPS[j][1] * P)
-            nc.vector.scalar_tensor_tensor(updated[:, cols], placed[:, cols], row_factor[:], base_banks[j][:], ALU.mult, ALU.add)
+        nc.scalar.mul(placed_scaled[:, OWN_SCALED:], placed[:, OWN_SCALED:BANK], row_factor[:])
+        nc.gpsimd.tensor_tensor(updated[:, :BANK], placed_scaled[:], base_direct[:], ALU.add)
+        for k in TURNED:
+            cols = slice(k * BANK, (k + 1) * BANK)
+            nc.vector.scalar_tensor_tensor(updated[:, cols], placed[:, cols], row_factor[:], base_banks[k][:], ALU.mult, ALU.add)
         half_cand = J // 2 // LIST_ROWS
         picked_lo = sb.tile([P, J // 2], F32)
         nc.vector.tensor_tensor(picked_lo[:], updated[:].indirect(candidates[:, :half_cand]), twos[:], ALU.mult)

@@ -74,7 +74,8 @@ def tile_attend_evictscores_kernel(tc, query, keys_words, keys_scales, mass, dec
         zeros = sb.tile([P, FIRST_SLOTS], F32)
         nc.gpsimd.memset(zeros[:], 0.0)
         placed = sb.tile([P, T], F32)
-        nc.vector.memset(placed[:], 0.0)
+        for k in range(QUARTERS):
+            nc.vector.memset(placed[:, k * BANK : (k + 1) * BANK], 0.0)
 
         late = held.tile([P, 12 * P + 1], F32, offset=0)
         mass_last = held.tile([P, BANK], F32, offset=LAST_AT)

@@ -54,7 +54,7 @@ def tile_attend_evictscores_kernel(tc, query, keys_words, keys_scales, mass, dec
         nc.sync.dma_start(word_pool[:].bitcast(I32), keys_words[0].bitcast(I32))
         candidates = sb.tile([P, J // LIST_ROWS], U16)
         nc.sync.dma_start(candidates[:], offs2)
-        query_raw = sb.tile([P, PACK, Q], F32)
+        query_raw = sb.tile([P, PACK, Q], F32, align_bytes=64, tag="query_raw")
         nc.sync.dma_start(query_raw[:], query.rearrange("(p j) q -> p j q", j=PACK))
         scale_pool = sb.tile([P, T], U8, align_bytes=64, tag="scale_pool")
         nc.vector.memset(scale_pool[:].bitcast(I32), 0)
@@ -91,14 +91,14 @@ def tile_attend_evictscores_kernel(tc, query, keys_words, keys_scales, mass, dec
         credit_turned = credit_banks[:, :P]
         nc.tensor.transpose(credit_turned, credit_rows[:], identity[:])
         debit = credit_turned[:, FIRST_CREDIT_ROW:]
-        debit_first = sb.tile([P, 3], F32, align_bytes=64, tag="debit_first")
-        nc.scalar.mul(debit_first[:], debit[:, 1:BLOCKS], minus_one[:])
+        debit_first = sb.tile([P, 2], F32, align_bytes=64, tag="debit_first")
+        nc.scalar.mul(debit_first[:], debit[:, 2:BLOCKS], minus_one[:])
         debit_rest = sb.tile([P, CREDIT_ROWS - BLOCKS], F32)
         nc.scalar.mul(debit_rest[:], debit[:, BLOCKS:], minus_one[:])
         H = I // 2
         front_lo = ps.tile([P, BANK], F32, offset=BANK_BYTES)
         front_hi = ps.tile([P, BANK], F32, offset=0)
-        for i, spread in enumerate((front_hi[:, H : H + P], front_hi[:, H + P :], front_lo[:, H : H + P])):
+        for i, spread in enumerate((front_hi[:, 3 * P :], front_lo[:, H : H + P])):
             nc.tensor.transpose(spread, debit_first[:, i : i + 1].to_broadcast([P, P]), identity[:])
 
         base_banks = {}
@@ -130,26 +130,30 @@ def tile_attend_evictscores_kernel(tc, query, keys_words, keys_scales, mass, dec
             scales=query_scales[:],
             in_=query_bf[:].rearrange("p q j -> p (q j)"),
         )
-        key_scales_hi = sb.tile([P, H], U8, align_bytes=64, tag="query_bf")
+        key_scales_hi = sb.tile([P, H], U8, align_bytes=64, tag="query_raw")
         nc.vector.tensor_copy(key_scales_hi[:], scale_pool[:].indirect(lists[1]))
-        score_banks = []
-        for half, key_scales in enumerate((key_scales_lo, key_scales_hi)):
-            scores = (front_lo, front_hi)[half][:, :H]
+        cut = P + P // 2
+        passes = (
+            (front_lo[:, :P], 0, P, key_scales_lo[:, :P]),
+            (front_lo[:, P:cut], P, cut, key_scales_lo[:, P:cut]),
+            (front_hi[:, : H - cut], cut, H, key_scales_lo[:, cut:]),
+            (front_hi[:, H - cut : I - cut], H, I, key_scales_hi[:]),
+        )
+        for scores, first, last, key_scales in passes:
             nc.tensor.matmul_mx(
                 out=scores,
                 lhsT=query_codes[:].bitcast(FP8X4),
                 lhsT_scale=query_scales[:],
-                rhs=key_words[:, half * H : (half + 1) * H].bitcast(FP4X4),
-                rhs_scale=key_scales[:],
+                rhs=key_words[:, first:last].bitcast(FP4X4),
+                rhs_scale=key_scales,
                 start=True,
                 stop=True,
             )
-            score_banks.append(scores)
         neg_scores = sb.tile([P, I], F32)
         neg_max_lo = sb.tile([P, 1], F32)
-        nc.vector.tensor_scalar(neg_scores[:, :H], score_banks[0], -1.0, None, ALU.mult, ALU.min, accum_out=neg_max_lo[:])
+        nc.vector.tensor_scalar(neg_scores[:, :cut], front_lo[:, :cut], -1.0, None, ALU.mult, ALU.min, accum_out=neg_max_lo[:])
         neg_max = sb.tile([P, 1], F32, tag="decayed_late")
-        nc.vector.tensor_scalar(neg_scores[:, H:], score_banks[1], -1.0, neg_max_lo[:], ALU.mult, ALU.min, accum_out=neg_max[:])
+        nc.vector.tensor_scalar(neg_scores[:, cut:], front_hi[:, : I - cut], -1.0, neg_max_lo[:], ALU.mult, ALU.min, accum_out=neg_max[:])
 
         base_direct = sb.tile([P, GPSIMD_COLS], F32)
 
@@ -158,12 +162,13 @@ def tile_attend_evictscores_kernel(tc, query, keys_words, keys_scales, mass, dec
                 base_direct[:, first:last], late[:, first:last], decay, spread, ALU.mult, ALU.add
             )
 
-        direct_base(P, P + H, front_hi[:, H:])
-        debit_last = sb.tile([P, 1], F32, align_bytes=64, tag="key_scales_lo")
-        nc.scalar.mul(debit_last[:], debit[:, :1], -1.0)
-        spread_late = ps.tile([P, P], F32, offset=2 * BANK_BYTES)
-        nc.tensor.transpose(spread_late[:], debit_last[:].to_broadcast([P, P]), identity[:])
-        direct_base(0, P, spread_late[:])
+        direct_base(H, H + P, front_hi[:, 3 * P :])
+        debit_last = sb.tile([P, 2], F32, align_bytes=64, tag="key_scales_lo")
+        nc.scalar.mul(debit_last[:], debit[:, :2], -1.0)
+        spread_late = ps.tile([P, H], F32, offset=2 * BANK_BYTES)
+        for i in range(2):
+            nc.tensor.transpose(spread_late[:, i * P : (i + 1) * P], debit_last[:, i : i + 1].to_broadcast([P, P]), identity[:])
+        direct_base(0, H, spread_late[:])
         decayed_early = sb.tile([P, T - EARLY], F32, align_bytes=64, tag="scale_pool")
         nc.gpsimd.tensor_scalar(decayed_early[:], mass_early, decay, 0.0, ALU.mult, ALU.add)
 

@@ -151,7 +151,8 @@ def tile_attend_evictscores_kernel(tc, query, keys_words, keys_scales, mass, dec
             )
         neg_scores = sb.tile([P, I], F32)
         neg_max_lo = sb.tile([P, 1], F32)
-        nc.vector.tensor_scalar(neg_scores[:, :cut], front_lo[:, :cut], -1.0, None, ALU.mult, ALU.min, accum_out=neg_max_lo[:])
+        nc.vector.tensor_reduce(neg_max_lo[:], front_lo[:, :cut], mybir.AxisListType.X, ALU.max, negate=True)
+        nc.scalar.mul(neg_scores[:, FIRST_SLOTS:cut], front_lo[:, FIRST_SLOTS:cut], -1.0)
         neg_max = sb.tile([P, 1], F32, tag="decayed_late")
         nc.vector.tensor_scalar(neg_scores[:, cut:], front_hi[:, : I - cut], -1.0, neg_max_lo[:], ALU.mult, ALU.min, accum_out=neg_max[:])
 

@@ -16,6 +16,7 @@ CREDIT_ROWS = T // P
 FIRST_CREDIT_ROW = P - CREDIT_ROWS
 WEIGHT_SCALE = 512.0
 GPSIMD_COLS = 512
+SHARE = 464
 OWN_SCALED = 224
 FIRST_SLOTS = 64
 LAST_AT = 12 * P * 4 + 32
@@ -209,12 +210,14 @@ def tile_attend_evictscores_kernel(tc, query, keys_words, keys_scales, mass, dec
                 )
 
         updated = sb.tile([P, T], F32)
-        placed_scaled = sb.tile([P, GPSIMD_COLS], F32, tag="decayed_late")
+        rest = slice(SHARE, BANK)
+        nc.vector.scalar_tensor_tensor(updated[:, rest], placed[:, rest], row_factor[:], base_direct[:, rest], ALU.mult, ALU.add)
+        placed_scaled = sb.tile([P, SHARE], F32, tag="decayed_late")
         nc.gpsimd.tensor_scalar(
             placed_scaled[:, :OWN_SCALED], placed[:, :OWN_SCALED], row_factor[:], 0.0, ALU.mult, ALU.add
         )
-        nc.scalar.mul(placed_scaled[:, OWN_SCALED:], placed[:, OWN_SCALED:BANK], row_factor[:])
-        nc.gpsimd.tensor_tensor(updated[:, :BANK], placed_scaled[:], base_direct[:], ALU.add)
+        nc.scalar.mul(placed_scaled[:, OWN_SCALED:], placed[:, OWN_SCALED:SHARE], row_factor[:])
+        nc.gpsimd.tensor_tensor(updated[:, :SHARE], placed_scaled[:], base_direct[:, :SHARE], ALU.add)
         for k in TURNED:
             cols = slice(k * BANK, (k + 1) * BANK)
             nc.vector.scalar_tensor_tensor(updated[:, cols], placed[:, cols], row_factor[:], base_banks[k][:], ALU.mult, ALU.add)

@@ -14,14 +14,14 @@ QUARTERS = T // BANK
 BANK_BYTES = 4 * BANK
 CREDIT_ROWS = T // P
 FIRST_CREDIT_ROW = P - CREDIT_ROWS
+DECAY_ROW = FIRST_CREDIT_ROW - 1
 WEIGHT_SCALE = 512.0
-GPSIMD_COLS = 512
-SHARE = 464
-OWN_SCALED = 224
-FIRST_SLOTS = 64
-LAST_AT = 12 * P * 4 + 32
-EARLY = T - 5 * P
-TURNED = (3, 1, 2)
+HEADROOM = 64.0
+H = I // 2
+SHARE = 448
+OWN_SCALED = 208
+TURNED = (1, 2, 3)
+MASS_ORDER = (1, 0, 2, 3)
 
 F32 = mybir.dt.float32
 BF16 = mybir.dt.bfloat16
@@ -33,6 +33,7 @@ FP8X4 = mybir.dt.float8_e4m3fn_x4
 FP4X4 = mybir.dt.float4_e2m1fn_x4
 ALU = mybir.AluOpType
 ACT = mybir.ActivationFunctionType
+AXIS_X = mybir.AxisListType.X
 
 FLOPS = 2 * D * Q * I
 
@@ -42,29 +43,29 @@ def tile_attend_evictscores_kernel(tc, query, keys_words, keys_scales, mass, dec
     with ExitStack() as ctx:
         sb = ctx.enter_context(tc.tile_pool(name="sb", bufs=1))
         held = ctx.enter_context(tc.tile_pool(name="held", bufs=1))
+        lay = ctx.enter_context(tc.tile_pool(name="lay", bufs=1))
         ps = ctx.enter_context(tc.psum_pool(name="ps", bufs=1))
 
         slots = sb.tile([P, I // LIST_ROWS], U16)
         nc.sync.dma_start(slots[:], offs)
+        query_raw = sb.tile([P, PACK, Q], F32, align_bytes=64)
+        nc.sync.dma_start(query_raw[:], query.rearrange("(p j) q -> p j q", j=PACK))
         credit_rows = sb.tile([P, P], F32)
         nc.scalar.dma_start(credit_rows[FIRST_CREDIT_ROW:, :], credit.rearrange("o (c p) -> (o c) p", p=P))
-        nc.gpsimd.memset(credit_rows[:FIRST_CREDIT_ROW, :], 0.0)
-        minus_one = sb.tile([P, 1], F32, align_bytes=64, tag="query_bf")
-        nc.gpsimd.memset(minus_one[:], -1.0)
-        word_pool = sb.tile([P, T], U16, align_bytes=64, tag="word_pool")
+        nc.scalar.dma_start(credit_rows[DECAY_ROW:FIRST_CREDIT_ROW, :], dec.rearrange("q o -> o q"))
+        nc.gpsimd.memset(credit_rows[:DECAY_ROW, :], 0.0)
+        word_pool = sb.tile([P, T], U16, align_bytes=64)
         nc.sync.dma_start(word_pool[:].bitcast(I32), keys_words[0].bitcast(I32))
         candidates = sb.tile([P, J // LIST_ROWS], U16)
         nc.sync.dma_start(candidates[:], offs2)
-        query_raw = sb.tile([P, PACK, Q], F32, align_bytes=64, tag="query_raw")
-        nc.sync.dma_start(query_raw[:], query.rearrange("(p j) q -> p j q", j=PACK))
-        scale_pool = sb.tile([P, T], U8, align_bytes=64, tag="scale_pool")
+        scale_pool = sb.tile([P, T], U8, align_bytes=64)
         nc.vector.memset(scale_pool[:].bitcast(I32), 0)
         for row in range(SCALE_ROWS):
             nc.sync.dma_start(
                 scale_pool[row:P:QUADRANT, :].bitcast(I32), keys_scales[0, row::SCALE_ROWS, :].bitcast(I32)
             )
-        ones = held.tile([P, P], F32, offset=LAST_AT - 256)
-        nc.vector.memset(ones[:], 1.0)
+        ones = sb.tile([P, P], F32)
+        nc.gpsimd.memset(ones[:], 1.0)
         identity = sb.tile([P, P], F32)
         nc.gpsimd.affine_select(
             out=identity[:], in_=ones[:], pattern=[[-1, P]], compare_op=ALU.is_equal, fill=0.0, base=0,
@@ -72,147 +73,128 @@ def tile_attend_evictscores_kernel(tc, query, keys_words, keys_scales, mass, dec
         )
         twos = sb.tile([P, J // 2], F32)
         nc.gpsimd.memset(twos[:], 2.0)
-        zeros = sb.tile([P, FIRST_SLOTS], F32)
-        nc.gpsimd.memset(zeros[:], 0.0)
+        minus_one = sb.tile([P, 1], F32)
+        nc.gpsimd.memset(minus_one[:], -1.0)
         placed = sb.tile([P, T], F32)
         for k in range(QUARTERS):
             nc.vector.memset(placed[:, k * BANK : (k + 1) * BANK], 0.0)
 
-        late = held.tile([P, 12 * P + 1], F32, offset=0)
-        mass_last = held.tile([P, BANK], F32, offset=LAST_AT)
-        mass_early = late[:, 7 * P : 12 * P]
-        decay = late[:, 12 * P :]
-        nc.sync.dma_start(decay, dec)
-        nc.sync.dma_start(mass_early, mass[:, EARLY:])
-        nc.sync.dma_start(late[:, : 3 * P], mass[:, : 3 * P])
-        nc.sync.dma_start(late[:, 3 * P : 7 * P], mass[:, 3 * P : 7 * P])
-        nc.sync.dma_start(mass_last[:], mass[:, 7 * P : EARLY])
-
-        credit_banks = ps.tile([P, 2 * BANK], F32, offset=6 * BANK_BYTES)
-        credit_turned = credit_banks[:, :P]
-        nc.tensor.transpose(credit_turned, credit_rows[:], identity[:])
-        debit = credit_turned[:, FIRST_CREDIT_ROW:]
-        debit_first = sb.tile([P, 2], F32, align_bytes=64, tag="debit_first")
-        nc.scalar.mul(debit_first[:], debit[:, 2:BLOCKS], minus_one[:])
-        debit_rest = sb.tile([P, CREDIT_ROWS - BLOCKS], F32)
-        nc.scalar.mul(debit_rest[:], debit[:, BLOCKS:], minus_one[:])
-        H = I // 2
-        front_lo = ps.tile([P, BANK], F32, offset=BANK_BYTES)
-        front_hi = ps.tile([P, BANK], F32, offset=0)
-        for i, spread in enumerate((front_hi[:, 3 * P :], front_lo[:, H : H + P])):
-            nc.tensor.transpose(spread, debit_first[:, i : i + 1].to_broadcast([P, P]), identity[:])
-
+        credit_bank = ps.tile([P, BANK], F32, offset=0)
+        nc.tensor.transpose(credit_bank[:, :P], credit_rows[:], identity[:])
+        columns = sb.tile([P, 1 + CREDIT_ROWS], F32)
+        nc.scalar.copy(columns[:], credit_bank[:, DECAY_ROW:P])
+        decay = columns[:, :1]
+        decay_bank = ps.tile([P, BANK], F32, offset=7 * BANK_BYTES)
+        nc.tensor.transpose(decay_bank[:, :P], decay.to_broadcast([P, P]), identity[:])
         base_banks = {}
-        for j, k in enumerate(TURNED):
-            base_bank = ps.tile([P, BANK], F32, offset=(3 + j) * BANK_BYTES, name="base_bank%d" % k)
+
+        def spread_credit(k, bank):
+            base_bank = ps.tile([P, BANK], F32, offset=bank * BANK_BYTES, name="base_bank%d" % k)
             for i in range(BLOCKS):
-                c = (k - 1) * BLOCKS + i
+                c = 1 + k * BLOCKS + i
                 nc.tensor.matmul(
-                    base_bank[:, i * P : (i + 1) * P], debit_rest[:, c : c + 1].to_broadcast([P, P]),
-                    identity[:], is_transpose=True, start=i == 0, stop=False,
+                    base_bank[:, i * P : (i + 1) * P], columns[:, c : c + 1].to_broadcast([P, P]), identity[:],
+                    is_transpose=True, start=i == 0, stop=k == 0 and i == BLOCKS - 1,
                 )
             base_banks[k] = base_bank
 
-        half_list = I // 2 // LIST_ROWS
-        lists = [slots[:, :half_list], slots[:, half_list:]]
-        key_words = sb.tile([P, I], U16, align_bytes=64)
-        nc.vector.tensor_copy(key_words[:], word_pool[:].indirect(slots[:]))
-        key_scales_lo = sb.tile([P, H], U8, align_bytes=64, tag="key_scales_lo")
-        nc.vector.tensor_copy(key_scales_lo[:], scale_pool[:].indirect(lists[0]))
-        query_bf = sb.tile([P, Q, PACK], BF16, align_bytes=64, tag="query_bf")
-        nc.scalar.copy(
+        for k in range(QUARTERS - 1):
+            spread_credit(k, 4 + k)
+
+        query_bf = held.tile([P, Q, PACK], BF16, offset=0, align_bytes=64)
+        nc.vector.tensor_copy(
             query_bf[:].rearrange("p (c i) j -> p c j i", i=PACK),
             query_raw[:].rearrange("p j (c i) -> p c j i", i=PACK),
         )
-        query_codes = sb.tile([P, Q], U32, align_bytes=64, tag="word_pool")
-        query_scales = sb.tile([P, Q], U8, align_bytes=64, tag="debit_first")
+        query_codes = sb.tile([P, Q], U32, align_bytes=64)
+        query_scales = sb.tile([P, Q], U8, align_bytes=64)
         nc.vector.quantize_mx(
             out=query_codes[:].bitcast(FP8X4),
             scales=query_scales[:],
             in_=query_bf[:].rearrange("p q j -> p (q j)"),
         )
-        key_scales_hi = sb.tile([P, H], U8, align_bytes=64, tag="query_raw")
-        nc.vector.tensor_copy(key_scales_hi[:], scale_pool[:].indirect(lists[1]))
-        cut = P + P // 2
-        passes = (
-            (front_lo[:, :P], 0, P, key_scales_lo[:, :P]),
-            (front_lo[:, P:cut], P, cut, key_scales_lo[:, P:cut]),
-            (front_hi[:, : H - cut], cut, H, key_scales_lo[:, cut:]),
-            (front_hi[:, H - cut : I - cut], H, I, key_scales_hi[:]),
-        )
-        for scores, first, last, key_scales in passes:
+        mass_sb = held.tile([P, T], F32, offset=0, align_bytes=64)
+        for k in MASS_ORDER:
+            nc.sync.dma_start(mass_sb[:, k * BANK : (k + 1) * BANK], mass[:, k * BANK : (k + 1) * BANK])
+
+        half_list = H // LIST_ROWS
+
+        lists = [slots[:, :half_list], slots[:, half_list:]]
+
+        def gather_words(half):
+            key_words = lay.tile([P, H], U16, align_bytes=64, offset=4 * P - 64 + 64 * half, name="key_words%d" % half)
+            nc.vector.tensor_copy(key_words[:], word_pool[:].indirect(lists[half]))
+            return key_words
+
+        def gather_scales(half):
+            key_scales = sb.tile([P, H], U8, align_bytes=64, tag="key_scales%d" % half, name="key_scales%d" % half)
+            nc.vector.tensor_copy(key_scales[:], scale_pool[:].indirect(lists[half]))
+            return key_scales
+
+        def scores_of(key_words, key_scales, scores):
             nc.tensor.matmul_mx(
                 out=scores,
                 lhsT=query_codes[:].bitcast(FP8X4),
                 lhsT_scale=query_scales[:],
-                rhs=key_words[:, first:last].bitcast(FP4X4),
-                rhs_scale=key_scales,
+                rhs=key_words[:].bitcast(FP4X4),
+                rhs_scale=key_scales[:],
                 start=True,
                 stop=True,
             )
-        neg_scores = sb.tile([P, I], F32)
+
+        def place(half, entries, source, sign, neg_shift):
+            weights = sb.tile([P, H], F32, name="weights%d" % half)
+            part_sum = sb.tile([P, 1], F32, name="part_sum%d" % half)
+            nc.scalar.activation(weights[:], source, ACT.Exp, bias=neg_shift[:], scale=sign, accum_out=part_sum[:])
+            nc.scalar.activation(placed[:].indirect(entries), weights[:], ACT.Copy)
+            return part_sum
+
+        scores_lo = ps.tile([P, H], F32, offset=0)
+        scores_of(gather_words(0), gather_scales(0), scores_lo[:])
+        scales_hi = gather_scales(1)
         neg_max_lo = sb.tile([P, 1], F32)
-        nc.vector.tensor_reduce(neg_max_lo[:], front_lo[:, :cut], mybir.AxisListType.X, ALU.max, negate=True)
-        nc.scalar.mul(neg_scores[:, FIRST_SLOTS:cut], front_lo[:, FIRST_SLOTS:cut], -1.0)
-        neg_max = sb.tile([P, 1], F32, tag="decayed_late")
-        nc.vector.tensor_scalar(neg_scores[:, cut:], front_hi[:, : I - cut], -1.0, neg_max_lo[:], ALU.mult, ALU.min, accum_out=neg_max[:])
-
-        base_direct = sb.tile([P, GPSIMD_COLS], F32)
-
-        def direct_base(first, last, spread):
-            nc.vector.scalar_tensor_tensor(
-                base_direct[:, first:last], late[:, first:last], decay, spread, ALU.mult, ALU.add
-            )
-
-        direct_base(H, H + P, front_hi[:, 3 * P :])
-        debit_last = sb.tile([P, 2], F32, align_bytes=64, tag="key_scales_lo")
-        nc.scalar.mul(debit_last[:], debit[:, :2], -1.0)
-        spread_late = ps.tile([P, H], F32, offset=2 * BANK_BYTES)
-        for i in range(2):
-            nc.tensor.transpose(spread_late[:, i * P : (i + 1) * P], debit_last[:, i : i + 1].to_broadcast([P, P]), identity[:])
-        direct_base(0, H, spread_late[:])
-        decayed_early = sb.tile([P, T - EARLY], F32, align_bytes=64, tag="scale_pool")
-        nc.gpsimd.tensor_scalar(decayed_early[:], mass_early, decay, 0.0, ALU.mult, ALU.add)
-
-        weights = sb.tile([P, I], F32)
-        first_cols = FIRST_SLOTS // LIST_ROWS
-        sum_first = sb.tile([P, 1], F32)
-        nc.scalar.activation(
-            weights[:, :FIRST_SLOTS], front_lo[:, :FIRST_SLOTS], ACT.Exp, bias=neg_max[:], accum_out=sum_first[:]
-        )
-        sum_rest = sb.tile([P, 1], F32)
-        nc.scalar.activation(
-            weights[:, FIRST_SLOTS:], neg_scores[:, FIRST_SLOTS:], ACT.Exp, bias=neg_max[:], scale=-1.0, accum_out=sum_rest[:]
-        )
-        nc.vector.tensor_tensor(placed[:].indirect(slots[:, :first_cols]), weights[:, :FIRST_SLOTS], zeros[:], ALU.add)
-        direct_base(H + P, BANK, front_lo[:, H : H + P])
+        nc.vector.tensor_reduce(neg_max_lo[:], scores_lo[:], AXIS_X, ALU.max, negate=True)
+        neg_decay_row = lay.tile([P, 1, P], F32, offset=0, align_bytes=64)
+        nc.scalar.mul(neg_decay_row[:, 0, :], decay_bank[:, :P], -1.0)
+        spread_credit(QUARTERS - 1, 7)
+        sum_lo = place(0, lists[0], scores_lo[:], 1.0, neg_max_lo)
+        banks_hi = ps.tile([P, 3 * BANK], F32, offset=BANK_BYTES)
+        scores_hi = banks_hi[:, 2 * BANK : 2 * BANK + H]
+        scores_of(gather_words(1), scales_hi, scores_hi)
+        neg_scores_hi = sb.tile([P, H], F32)
+        neg_max_hi = sb.tile([P, 1], F32)
+        nc.vector.tensor_scalar(neg_scores_hi[:], scores_hi, -1.0, None, ALU.mult, ALU.min, accum_out=neg_max_hi[:])
+        neg_shift_hi = sb.tile([P, 1], F32)
+        nc.gpsimd.tensor_scalar(neg_shift_hi[:], neg_max_hi[:], HEADROOM, neg_max_lo[:], ALU.add, ALU.min)
+        sum_hi = place(1, lists[1], neg_scores_hi[:], -1.0, neg_shift_hi)
         row_sum_scaled = sb.tile([P, 1], F32)
-        nc.vector.tensor_scalar(row_sum_scaled[:], sum_first[:], sum_rest[:], 1.0 / WEIGHT_SCALE, ALU.add, ALU.mult)
-        nc.vector.tensor_copy(placed[:].indirect(slots[:, first_cols:]), weights[:, FIRST_SLOTS:])
+        nc.gpsimd.tensor_scalar(row_sum_scaled[:], sum_lo[:], sum_hi[:], 1.0 / WEIGHT_SCALE, ALU.add, ALU.mult)
         row_factor = sb.tile([P, 1], F32)
-        nc.vector.reciprocal(row_factor[:], row_sum_scaled[:])
+        nc.gpsimd.tensor_tensor(row_factor[:], row_sum_scaled[:], minus_one[:], ALU.pow)
 
-        decayed_late = sb.tile([P, EARLY - BANK], F32, tag="decayed_late")
-        nc.scalar.mul(decayed_late[:, : 3 * P], late[:, BANK : 7 * P], decay)
-        nc.scalar.mul(decayed_late[:, 3 * P :], mass_last[:], decay)
-        for j, k in enumerate(TURNED):
-            turned_bank = ps.tile([P, BANK], F32, offset=(6, 0, 7)[j] * BANK_BYTES, name="turned%d" % k)
-            for i in reversed(range(BLOCKS)) if k == 2 else range(BLOCKS):
+        base_direct = sb.tile([P, BANK], F32, align_bytes=64, tag="key_scales1")
+        for k in MASS_ORDER:
+            if k == 0:
+                nc.vector.scalar_tensor_tensor(
+                    base_direct[:], mass_sb[:, :BANK], decay, base_banks[0][:], ALU.mult, ALU.subtract
+                )
+                continue
+            turned_bank = ps.tile([P, BLOCKS, P], F32, offset=(k - 1) * BANK_BYTES, name="turned%d" % k)
+            for i in range(BLOCKS):
                 first = k * BANK + i * P
-                source = decayed_early[:, first - EARLY : first - EARLY + P] if first >= EARLY else decayed_late[:, first - BANK : first - BANK + P]
-                nc.tensor.transpose(turned_bank[:, i * P : (i + 1) * P], source, identity[:])
-            base_turned = held.tile([P, BANK], F32, name="base_turned%d" % k, offset=LAST_AT + j * BANK_BYTES)
-            nc.scalar.copy(base_turned[:], turned_bank[:])
+                nc.tensor.transpose(turned_bank[:, i, :], mass_sb[:, first : first + P], identity[:])
+            base_turned = lay.tile([P, BLOCKS, P], F32, offset=4 * P + (k - 1) * BANK_BYTES, align_bytes=64, name="base_turned%d" % k)
+            nc.vector.tensor_tensor(base_turned[:], neg_decay_row[:].to_broadcast([P, BLOCKS, P]), turned_bank[:], ALU.mult)
             for i in range(BLOCKS):
                 nc.tensor.matmul(
-                    base_banks[k][:, i * P : (i + 1) * P], base_turned[:, i * P : (i + 1) * P], identity[:],
+                    base_banks[k][:, i * P : (i + 1) * P], base_turned[:, i, :], identity[:],
                     is_transpose=True, start=False, stop=i == BLOCKS - 1,
                 )
 
         updated = sb.tile([P, T], F32)
         rest = slice(SHARE, BANK)
         nc.vector.scalar_tensor_tensor(updated[:, rest], placed[:, rest], row_factor[:], base_direct[:, rest], ALU.mult, ALU.add)
-        placed_scaled = sb.tile([P, SHARE], F32, tag="decayed_late")
+        placed_scaled = sb.tile([P, SHARE], F32)
         nc.gpsimd.tensor_scalar(
             placed_scaled[:, :OWN_SCALED], placed[:, :OWN_SCALED], row_factor[:], 0.0, ALU.mult, ALU.add
         )
@@ -220,7 +202,7 @@ def tile_attend_evictscores_kernel(tc, query, keys_words, keys_scales, mass, dec
         nc.gpsimd.tensor_tensor(updated[:, :SHARE], placed_scaled[:], base_direct[:, :SHARE], ALU.add)
         for k in TURNED:
             cols = slice(k * BANK, (k + 1) * BANK)
-            nc.vector.scalar_tensor_tensor(updated[:, cols], placed[:, cols], row_factor[:], base_banks[k][:], ALU.mult, ALU.add)
+            nc.vector.scalar_tensor_tensor(updated[:, cols], placed[:, cols], row_factor[:], base_banks[k][:], ALU.mult, ALU.subtract)
         half_cand = J // 2 // LIST_ROWS
         picked_lo = sb.tile([P, J // 2], F32)
         nc.vector.tensor_tensor(picked_lo[:], updated[:].indirect(candidates[:, :half_cand]), twos[:], ALU.mult)

@@ -14,14 +14,13 @@ QUARTERS = T // BANK
 BANK_BYTES = 4 * BANK
 CREDIT_ROWS = T // P
 FIRST_CREDIT_ROW = P - CREDIT_ROWS
-DECAY_ROW = FIRST_CREDIT_ROW - 1
 WEIGHT_SCALE = 512.0
 HEADROOM = 64.0
 H = I // 2
 SHARE = 448
 OWN_SCALED = 208
 TURNED = (1, 2, 3)
-MASS_ORDER = (1, 0, 2, 3)
+FIRST_SLOTS = 160
 
 F32 = mybir.dt.float32
 BF16 = mybir.dt.bfloat16
@@ -43,29 +42,29 @@ def tile_attend_evictscores_kernel(tc, query, keys_words, keys_scales, mass, dec
     with ExitStack() as ctx:
         sb = ctx.enter_context(tc.tile_pool(name="sb", bufs=1))
         held = ctx.enter_context(tc.tile_pool(name="held", bufs=1))
-        lay = ctx.enter_context(tc.tile_pool(name="lay", bufs=1))
         ps = ctx.enter_context(tc.psum_pool(name="ps", bufs=1))
 
         slots = sb.tile([P, I // LIST_ROWS], U16)
         nc.sync.dma_start(slots[:], offs)
-        query_raw = sb.tile([P, PACK, Q], F32, align_bytes=64)
-        nc.sync.dma_start(query_raw[:], query.rearrange("(p j) q -> p j q", j=PACK))
         credit_rows = sb.tile([P, P], F32)
         nc.scalar.dma_start(credit_rows[FIRST_CREDIT_ROW:, :], credit.rearrange("o (c p) -> (o c) p", p=P))
-        nc.scalar.dma_start(credit_rows[DECAY_ROW:FIRST_CREDIT_ROW, :], dec.rearrange("q o -> o q"))
-        nc.gpsimd.memset(credit_rows[:DECAY_ROW, :], 0.0)
-        word_pool = sb.tile([P, T], U16, align_bytes=64)
+        nc.gpsimd.memset(credit_rows[:FIRST_CREDIT_ROW, :], 0.0)
+        minus_one = sb.tile([P, 1], F32, align_bytes=64, tag="query_bf")
+        nc.gpsimd.memset(minus_one[:], -1.0)
+        word_pool = sb.tile([P, T], U16, align_bytes=64, tag="word_pool")
         nc.sync.dma_start(word_pool[:].bitcast(I32), keys_words[0].bitcast(I32))
         candidates = sb.tile([P, J // LIST_ROWS], U16)
         nc.sync.dma_start(candidates[:], offs2)
+        query_raw = sb.tile([P, PACK, Q], F32, align_bytes=64, tag="query_raw")
+        nc.sync.dma_start(query_raw[:], query.rearrange("(p j) q -> p j q", j=PACK))
         scale_pool = sb.tile([P, T], U8, align_bytes=64)
         nc.vector.memset(scale_pool[:].bitcast(I32), 0)
         for row in range(SCALE_ROWS):
             nc.sync.dma_start(
                 scale_pool[row:P:QUADRANT, :].bitcast(I32), keys_scales[0, row::SCALE_ROWS, :].bitcast(I32)
             )
-        ones = sb.tile([P, P], F32)
-        nc.gpsimd.memset(ones[:], 1.0)
+        ones = held.tile([P, P], F32, offset=0)
+        nc.vector.memset(ones[:], 1.0)
         identity = sb.tile([P, P], F32)
         nc.gpsimd.affine_select(
             out=identity[:], in_=ones[:], pattern=[[-1, P]], compare_op=ALU.is_equal, fill=0.0, base=0,
@@ -73,125 +72,122 @@ def tile_attend_evictscores_kernel(tc, query, keys_words, keys_scales, mass, dec
         )
         twos = sb.tile([P, J // 2], F32)
         nc.gpsimd.memset(twos[:], 2.0)
-        minus_one = sb.tile([P, 1], F32)
-        nc.gpsimd.memset(minus_one[:], -1.0)
+        zeros = sb.tile([P, FIRST_SLOTS], F32)
+        nc.gpsimd.memset(zeros[:], 0.0)
         placed = sb.tile([P, T], F32)
         for k in range(QUARTERS):
             nc.vector.memset(placed[:, k * BANK : (k + 1) * BANK], 0.0)
+        late = held.tile([P, T + 1], F32, offset=0)
+        mass_sb = late[:, :T]
+        decay = late[:, T:]
+        nc.sync.dma_start(decay, dec)
+        nc.sync.dma_start(mass_sb[:, BANK:], mass[:, BANK:])
+        nc.sync.dma_start(mass_sb[:, :BANK], mass[:, :BANK])
 
         credit_bank = ps.tile([P, BANK], F32, offset=0)
         nc.tensor.transpose(credit_bank[:, :P], credit_rows[:], identity[:])
-        columns = sb.tile([P, 1 + CREDIT_ROWS], F32)
-        nc.scalar.copy(columns[:], credit_bank[:, DECAY_ROW:P])
-        decay = columns[:, :1]
-        decay_bank = ps.tile([P, BANK], F32, offset=7 * BANK_BYTES)
-        nc.tensor.transpose(decay_bank[:, :P], decay.to_broadcast([P, P]), identity[:])
+        debit = sb.tile([P, CREDIT_ROWS], F32)
+        nc.scalar.mul(debit[:], credit_bank[:, FIRST_CREDIT_ROW:P], minus_one[:])
         base_banks = {}
 
-        def spread_credit(k, bank):
+        def spread_debit(k, bank):
             base_bank = ps.tile([P, BANK], F32, offset=bank * BANK_BYTES, name="base_bank%d" % k)
             for i in range(BLOCKS):
-                c = 1 + k * BLOCKS + i
+                c = k * BLOCKS + i
                 nc.tensor.matmul(
-                    base_bank[:, i * P : (i + 1) * P], columns[:, c : c + 1].to_broadcast([P, P]), identity[:],
+                    base_bank[:, i * P : (i + 1) * P], debit[:, c : c + 1].to_broadcast([P, P]), identity[:],
                     is_transpose=True, start=i == 0, stop=k == 0 and i == BLOCKS - 1,
                 )
             base_banks[k] = base_bank
 
         for k in range(QUARTERS - 1):
-            spread_credit(k, 4 + k)
+            spread_debit(k, 4 + k)
 
-        query_bf = held.tile([P, Q, PACK], BF16, offset=0, align_bytes=64)
-        nc.vector.tensor_copy(
+        half_list = H // LIST_ROWS
+        key_words = sb.tile([P, I], U16, align_bytes=64)
+        nc.vector.tensor_copy(key_words[:], word_pool[:].indirect(slots[:]))
+        key_scales_lo = sb.tile([P, H], U8, align_bytes=64)
+        nc.vector.tensor_copy(key_scales_lo[:], scale_pool[:].indirect(slots[:, :half_list]))
+        query_bf = sb.tile([P, Q, PACK], BF16, align_bytes=64, tag="query_bf")
+        nc.scalar.copy(
             query_bf[:].rearrange("p (c i) j -> p c j i", i=PACK),
             query_raw[:].rearrange("p j (c i) -> p c j i", i=PACK),
         )
-        query_codes = sb.tile([P, Q], U32, align_bytes=64)
+        query_codes = sb.tile([P, Q], U32, align_bytes=64, tag="word_pool")
         query_scales = sb.tile([P, Q], U8, align_bytes=64)
         nc.vector.quantize_mx(
             out=query_codes[:].bitcast(FP8X4),
             scales=query_scales[:],
             in_=query_bf[:].rearrange("p q j -> p (q j)"),
         )
-        mass_sb = held.tile([P, T], F32, offset=0, align_bytes=64)
-        for k in MASS_ORDER:
-            nc.sync.dma_start(mass_sb[:, k * BANK : (k + 1) * BANK], mass[:, k * BANK : (k + 1) * BANK])
+        key_scales_hi = sb.tile([P, H], U8, align_bytes=64, tag="query_raw")
+        nc.vector.tensor_copy(key_scales_hi[:], scale_pool[:].indirect(slots[:, half_list:]))
 
-        half_list = H // LIST_ROWS
-
-        lists = [slots[:, :half_list], slots[:, half_list:]]
-
-        def gather_words(half):
-            key_words = lay.tile([P, H], U16, align_bytes=64, offset=4 * P - 64 + 64 * half, name="key_words%d" % half)
-            nc.vector.tensor_copy(key_words[:], word_pool[:].indirect(lists[half]))
-            return key_words
-
-        def gather_scales(half):
-            key_scales = sb.tile([P, H], U8, align_bytes=64, tag="key_scales%d" % half, name="key_scales%d" % half)
-            nc.vector.tensor_copy(key_scales[:], scale_pool[:].indirect(lists[half]))
-            return key_scales
-
-        def scores_of(key_words, key_scales, scores):
+        def scores_of(first, key_scales, scores):
             nc.tensor.matmul_mx(
                 out=scores,
                 lhsT=query_codes[:].bitcast(FP8X4),
                 lhsT_scale=query_scales[:],
-                rhs=key_words[:].bitcast(FP4X4),
+                rhs=key_words[:, first : first + H].bitcast(FP4X4),
                 rhs_scale=key_scales[:],
                 start=True,
                 stop=True,
             )
 
-        def place(half, entries, source, sign, neg_shift):
-            weights = sb.tile([P, H], F32, name="weights%d" % half)
-            part_sum = sb.tile([P, 1], F32, name="part_sum%d" % half)
-            nc.scalar.activation(weights[:], source, ACT.Exp, bias=neg_shift[:], scale=sign, accum_out=part_sum[:])
-            nc.scalar.activation(placed[:].indirect(entries), weights[:], ACT.Copy)
-            return part_sum
-
         scores_lo = ps.tile([P, H], F32, offset=0)
-        scores_of(gather_words(0), gather_scales(0), scores_lo[:])
-        scales_hi = gather_scales(1)
+        scores_of(0, key_scales_lo, scores_lo[:])
+        decay_bank = ps.tile([P, BANK], F32, offset=7 * BANK_BYTES)
+        nc.tensor.transpose(decay_bank[:, :P], decay.to_broadcast([P, P]), identity[:])
+        decay_row = sb.tile([P, 1, P], F32)
+        nc.scalar.copy(decay_row[:, 0, :], decay_bank[:, :P])
+        banks_hi = ps.tile([P, 3 * BANK], F32, offset=BANK_BYTES)
+        scores_hi = banks_hi[:, :H]
+        scores_of(H, key_scales_hi, scores_hi)
+        spread_debit(QUARTERS - 1, 7)
+
         neg_max_lo = sb.tile([P, 1], F32)
         nc.vector.tensor_reduce(neg_max_lo[:], scores_lo[:], AXIS_X, ALU.max, negate=True)
-        neg_decay_row = lay.tile([P, 1, P], F32, offset=0, align_bytes=64)
-        nc.scalar.mul(neg_decay_row[:, 0, :], decay_bank[:, :P], -1.0)
-        spread_credit(QUARTERS - 1, 7)
-        sum_lo = place(0, lists[0], scores_lo[:], 1.0, neg_max_lo)
-        banks_hi = ps.tile([P, 3 * BANK], F32, offset=BANK_BYTES)
-        scores_hi = banks_hi[:, 2 * BANK : 2 * BANK + H]
-        scores_of(gather_words(1), scales_hi, scores_hi)
-        neg_scores_hi = sb.tile([P, H], F32)
-        neg_max_hi = sb.tile([P, 1], F32)
-        nc.vector.tensor_scalar(neg_scores_hi[:], scores_hi, -1.0, None, ALU.mult, ALU.min, accum_out=neg_max_hi[:])
-        neg_shift_hi = sb.tile([P, 1], F32)
-        nc.gpsimd.tensor_scalar(neg_shift_hi[:], neg_max_hi[:], HEADROOM, neg_max_lo[:], ALU.add, ALU.min)
-        sum_hi = place(1, lists[1], neg_scores_hi[:], -1.0, neg_shift_hi)
+        above_hi = sb.tile([P, H], F32)
+        reach_hi = sb.tile([P, 1], F32, tag="reach_hi")
+        nc.vector.tensor_scalar(above_hi[:], scores_hi, neg_max_lo[:], HEADROOM, ALU.add, ALU.max, accum_out=reach_hi[:])
+        weights = sb.tile([P, I], F32)
+        part_sums = sb.tile([P, 3], F32)
+        for i, part in enumerate((slice(0, FIRST_SLOTS), slice(FIRST_SLOTS, H))):
+            nc.scalar.activation(
+                weights[:, part], scores_lo[:, part], ACT.Exp, bias=neg_max_lo[:], accum_out=part_sums[:, i : i + 1]
+            )
+        neg_excess_hi = sb.tile([P, 1], F32)
+        nc.scalar.activation(neg_excess_hi[:], reach_hi[:], ACT.Copy, bias=HEADROOM, scale=-1.0)
+        nc.scalar.activation(weights[:, H:], above_hi[:], ACT.Exp, bias=neg_excess_hi[:], accum_out=part_sums[:, 2:])
+        first_cols = FIRST_SLOTS // LIST_ROWS
+        nc.vector.tensor_tensor(placed[:].indirect(slots[:, :first_cols]), weights[:, :FIRST_SLOTS], zeros[:], ALU.add)
+        nc.scalar.activation(placed[:].indirect(slots[:, first_cols:]), weights[:, FIRST_SLOTS:], ACT.Copy)
         row_sum_scaled = sb.tile([P, 1], F32)
-        nc.gpsimd.tensor_scalar(row_sum_scaled[:], sum_lo[:], sum_hi[:], 1.0 / WEIGHT_SCALE, ALU.add, ALU.mult)
+        part_sums_scaled = sb.tile([P, 3], F32)
+        nc.vector.tensor_scalar(
+            part_sums_scaled[:], part_sums[:], 1.0 / WEIGHT_SCALE, None, ALU.mult, ALU.add, accum_out=row_sum_scaled[:]
+        )
         row_factor = sb.tile([P, 1], F32)
-        nc.gpsimd.tensor_tensor(row_factor[:], row_sum_scaled[:], minus_one[:], ALU.pow)
+        nc.vector.reciprocal(row_factor[:], row_sum_scaled[:])
 
-        base_direct = sb.tile([P, BANK], F32, align_bytes=64, tag="key_scales1")
-        for k in MASS_ORDER:
-            if k == 0:
-                nc.vector.scalar_tensor_tensor(
-                    base_direct[:], mass_sb[:, :BANK], decay, base_banks[0][:], ALU.mult, ALU.subtract
-                )
-                continue
-            turned_bank = ps.tile([P, BLOCKS, P], F32, offset=(k - 1) * BANK_BYTES, name="turned%d" % k)
+        base_direct = sb.tile([P, BANK], F32, tag="reach_hi")
+        nc.vector.scalar_tensor_tensor(base_direct[:], mass_sb[:, :BANK], decay, base_banks[0][:], ALU.mult, ALU.add)
+        turned_banks = {}
+        for k in TURNED:
+            turned_banks[k] = ps.tile([P, BLOCKS, P], F32, offset=k * BANK_BYTES, name="turned%d" % k)
             for i in range(BLOCKS):
                 first = k * BANK + i * P
-                nc.tensor.transpose(turned_bank[:, i, :], mass_sb[:, first : first + P], identity[:])
-            base_turned = lay.tile([P, BLOCKS, P], F32, offset=4 * P + (k - 1) * BANK_BYTES, align_bytes=64, name="base_turned%d" % k)
-            nc.vector.tensor_tensor(base_turned[:], neg_decay_row[:].to_broadcast([P, BLOCKS, P]), turned_bank[:], ALU.mult)
+                nc.tensor.transpose(turned_banks[k][:, i, :], mass_sb[:, first : first + P], identity[:])
+        for k in TURNED:
+            base_turned = sb.tile([P, BLOCKS, P], F32, name="base_turned%d" % k)
+            nc.vector.tensor_tensor(base_turned[:], decay_row[:].to_broadcast([P, BLOCKS, P]), turned_banks[k][:], ALU.mult)
             for i in range(BLOCKS):
                 nc.tensor.matmul(
                     base_banks[k][:, i * P : (i + 1) * P], base_turned[:, i, :], identity[:],
                     is_transpose=True, start=False, stop=i == BLOCKS - 1,
                 )
 
-        updated = sb.tile([P, T], F32)
+        updated = held.tile([P, T], F32, offset=0)
         rest = slice(SHARE, BANK)
         nc.vector.scalar_tensor_tensor(updated[:, rest], placed[:, rest], row_factor[:], base_direct[:, rest], ALU.mult, ALU.add)
         placed_scaled = sb.tile([P, SHARE], F32)
@@ -202,7 +198,7 @@ def tile_attend_evictscores_kernel(tc, query, keys_words, keys_scales, mass, dec
         nc.gpsimd.tensor_tensor(updated[:, :SHARE], placed_scaled[:], base_direct[:, :SHARE], ALU.add)
         for k in TURNED:
             cols = slice(k * BANK, (k + 1) * BANK)
-            nc.vector.scalar_tensor_tensor(updated[:, cols], placed[:, cols], row_factor[:], base_banks[k][:], ALU.mult, ALU.subtract)
+            nc.vector.scalar_tensor_tensor(updated[:, cols], placed[:, cols], row_factor[:], base_banks[k][:], ALU.mult, ALU.add)
         half_cand = J // 2 // LIST_ROWS
         picked_lo = sb.tile([P, J // 2], F32)
         nc.vector.tensor_tensor(picked_lo[:], updated[:].indirect(candidates[:, :half_cand]), twos[:], ALU.mult)

@@ -21,6 +21,7 @@ SHARE = 448
 OWN_SCALED = 208
 TURNED = (1, 2, 3)
 FIRST_SLOTS = 160
+EARLY_SPREADS = 2
 
 F32 = mybir.dt.float32
 BF16 = mybir.dt.bfloat16
@@ -84,7 +85,7 @@ def tile_attend_evictscores_kernel(tc, query, keys_words, keys_scales, mass, dec
         nc.sync.dma_start(mass_sb[:, BANK:], mass[:, BANK:])
         nc.sync.dma_start(mass_sb[:, :BANK], mass[:, :BANK])
 
-        credit_bank = ps.tile([P, BANK], F32, offset=0)
+        credit_bank = ps.tile([P, BANK], F32, offset=6 * BANK_BYTES)
         nc.tensor.transpose(credit_bank[:, :P], credit_rows[:], identity[:])
         debit = sb.tile([P, CREDIT_ROWS], F32)
         nc.scalar.mul(debit[:], credit_bank[:, FIRST_CREDIT_ROW:P], minus_one[:])
@@ -100,8 +101,8 @@ def tile_attend_evictscores_kernel(tc, query, keys_words, keys_scales, mass, dec
                 )
             base_banks[k] = base_bank
 
-        for k in range(QUARTERS - 1):
-            spread_debit(k, 4 + k)
+        for k in range(EARLY_SPREADS):
+            spread_debit(k, 3 + k)
 
         half_list = H // LIST_ROWS
         key_words = sb.tile([P, I], U16, align_bytes=64)
@@ -134,19 +135,15 @@ def tile_attend_evictscores_kernel(tc, query, keys_words, keys_scales, mass, dec
                 stop=True,
             )
 
-        scores_lo = ps.tile([P, H], F32, offset=0)
-        scores_of(0, key_scales_lo, scores_lo[:])
-        decay_bank = ps.tile([P, BANK], F32, offset=7 * BANK_BYTES)
-        nc.tensor.transpose(decay_bank[:, :P], decay.to_broadcast([P, P]), identity[:])
-        decay_row = sb.tile([P, 1, P], F32)
-        nc.scalar.copy(decay_row[:, 0, :], decay_bank[:, :P])
-        banks_hi = ps.tile([P, 3 * BANK], F32, offset=BANK_BYTES)
-        scores_hi = banks_hi[:, :H]
+        banks_lo = ps.tile([P, 3 * BANK], F32, offset=5 * BANK_BYTES)
+        scores_lo = banks_lo[:, :H]
+        scores_of(0, key_scales_lo, scores_lo)
+        bank_hi = ps.tile([P, H], F32, offset=0)
+        scores_hi = bank_hi[:]
         scores_of(H, key_scales_hi, scores_hi)
-        spread_debit(QUARTERS - 1, 7)
 
         neg_max_lo = sb.tile([P, 1], F32)
-        nc.vector.tensor_reduce(neg_max_lo[:], scores_lo[:], AXIS_X, ALU.max, negate=True)
+        nc.vector.tensor_reduce(neg_max_lo[:], scores_lo, AXIS_X, ALU.max, negate=True)
         above_hi = sb.tile([P, H], F32)
         reach_hi = sb.tile([P, 1], F32, tag="reach_hi")
         nc.vector.tensor_scalar(above_hi[:], scores_hi, neg_max_lo[:], HEADROOM, ALU.add, ALU.max, accum_out=reach_hi[:])
@@ -170,14 +167,20 @@ def tile_attend_evictscores_kernel(tc, query, keys_words, keys_scales, mass, dec
         row_factor = sb.tile([P, 1], F32)
         nc.vector.reciprocal(row_factor[:], row_sum_scaled[:])
 
+        decay_bank = ps.tile([P, BANK], F32, offset=7 * BANK_BYTES)
+        nc.tensor.transpose(decay_bank[:, :P], decay.to_broadcast([P, P]), identity[:])
+        decay_row = sb.tile([P, 1, P], F32)
+        nc.vector.tensor_copy(decay_row[:, 0, :], decay_bank[:, :P])
         base_direct = sb.tile([P, BANK], F32, tag="reach_hi")
         nc.vector.scalar_tensor_tensor(base_direct[:], mass_sb[:, :BANK], decay, base_banks[0][:], ALU.mult, ALU.add)
         turned_banks = {}
         for k in TURNED:
-            turned_banks[k] = ps.tile([P, BLOCKS, P], F32, offset=k * BANK_BYTES, name="turned%d" % k)
+            turned_banks[k] = ps.tile([P, BLOCKS, P], F32, offset=k % 3 * BANK_BYTES, name="turned%d" % k)
             for i in range(BLOCKS):
                 first = k * BANK + i * P
                 nc.tensor.transpose(turned_banks[k][:, i, :], mass_sb[:, first : first + P], identity[:])
+        for k in range(EARLY_SPREADS, QUARTERS):
+            spread_debit(k, 3 + k)
         for k in TURNED:
             base_turned = sb.tile([P, BLOCKS, P], F32, name="base_turned%d" % k)
             nc.vector.tensor_tensor(base_turned[:], decay_row[:].to_broadcast([P, BLOCKS, P]), turned_banks[k][:], ALU.mult)

@@ -58,7 +58,7 @@ def tile_attend_evictscores_kernel(tc, query, keys_words, keys_scales, mass, dec
         nc.sync.dma_start(candidates[:], offs2)
         query_raw = sb.tile([P, PACK, Q], F32, align_bytes=64, tag="query_raw")
         nc.sync.dma_start(query_raw[:], query.rearrange("(p j) q -> p j q", j=PACK))
-        scale_pool = sb.tile([P, T], U8, align_bytes=64)
+        scale_pool = sb.tile([P, T], U8, align_bytes=64, tag="scale_pool")
         nc.vector.memset(scale_pool[:].bitcast(I32), 0)
         for row in range(SCALE_ROWS):
             nc.sync.dma_start(
@@ -71,10 +71,6 @@ def tile_attend_evictscores_kernel(tc, query, keys_words, keys_scales, mass, dec
             out=identity[:], in_=ones[:], pattern=[[-1, P]], compare_op=ALU.is_equal, fill=0.0, base=0,
             channel_multiplier=1,
         )
-        twos = sb.tile([P, J // 2], F32)
-        nc.gpsimd.memset(twos[:], 2.0)
-        zeros = sb.tile([P, FIRST_SLOTS], F32)
-        nc.gpsimd.memset(zeros[:], 0.0)
         placed = sb.tile([P, T], F32)
         for k in range(QUARTERS):
             nc.vector.memset(placed[:, k * BANK : (k + 1) * BANK], 0.0)
@@ -156,13 +152,15 @@ def tile_attend_evictscores_kernel(tc, query, keys_words, keys_scales, mass, dec
         neg_excess_hi = sb.tile([P, 1], F32)
         nc.scalar.activation(neg_excess_hi[:], reach_hi[:], ACT.Copy, bias=HEADROOM, scale=-1.0)
         nc.scalar.activation(weights[:, H:], above_hi[:], ACT.Exp, bias=neg_excess_hi[:], accum_out=part_sums[:, 2:])
+        twos = sb.tile([P, J // 2], F32, align_bytes=64, tag="scale_pool")
+        nc.gpsimd.memset(twos[:], 2.0)
         first_cols = FIRST_SLOTS // LIST_ROWS
-        nc.vector.tensor_tensor(placed[:].indirect(slots[:, :first_cols]), weights[:, :FIRST_SLOTS], zeros[:], ALU.add)
-        nc.scalar.activation(placed[:].indirect(slots[:, first_cols:]), weights[:, FIRST_SLOTS:], ACT.Copy)
+        nc.vector.tensor_tensor(placed[:].indirect(slots[:, :first_cols]), weights[:, :FIRST_SLOTS], weights[:, :FIRST_SLOTS], ALU.add)
+        nc.scalar.activation(placed[:].indirect(slots[:, first_cols:]), weights[:, FIRST_SLOTS:], ACT.Copy, scale=2.0)
         row_sum_scaled = sb.tile([P, 1], F32)
         part_sums_scaled = sb.tile([P, 3], F32)
         nc.vector.tensor_scalar(
-            part_sums_scaled[:], part_sums[:], 1.0 / WEIGHT_SCALE, None, ALU.mult, ALU.add, accum_out=row_sum_scaled[:]
+            part_sums_scaled[:], part_sums[:], 2.0 / WEIGHT_SCALE, None, ALU.mult, ALU.add, accum_out=row_sum_scaled[:]
         )
         row_factor = sb.tile([P, 1], F32)
         nc.vector.reciprocal(row_factor[:], row_sum_scaled[:])

@@ -45,8 +45,6 @@ def tile_attend_evictscores_kernel(tc, query, keys_words, keys_scales, mass, dec
         held = ctx.enter_context(tc.tile_pool(name="held", bufs=1))
         ps = ctx.enter_context(tc.psum_pool(name="ps", bufs=1))
 
-        slots = sb.tile([P, I // LIST_ROWS], U16)
-        nc.sync.dma_start(slots[:], offs)
         credit_rows = sb.tile([P, P], F32)
         nc.scalar.dma_start(credit_rows[FIRST_CREDIT_ROW:, :], credit.rearrange("o (c p) -> (o c) p", p=P))
         nc.gpsimd.memset(credit_rows[:FIRST_CREDIT_ROW, :], 0.0)
@@ -54,8 +52,8 @@ def tile_attend_evictscores_kernel(tc, query, keys_words, keys_scales, mass, dec
         nc.gpsimd.memset(minus_one[:], -1.0)
         word_pool = sb.tile([P, T], U16, align_bytes=64, tag="word_pool")
         nc.sync.dma_start(word_pool[:].bitcast(I32), keys_words[0].bitcast(I32))
-        candidates = sb.tile([P, J // LIST_ROWS], U16)
-        nc.sync.dma_start(candidates[:], offs2)
+        slots = sb.tile([P, I // LIST_ROWS], U16)
+        nc.sync.dma_start(slots[:], offs)
         query_raw = sb.tile([P, PACK, Q], F32, align_bytes=64, tag="query_raw")
         nc.sync.dma_start(query_raw[:], query.rearrange("(p j) q -> p j q", j=PACK))
         scale_pool = sb.tile([P, T], U8, align_bytes=64, tag="scale_pool")
@@ -64,6 +62,8 @@ def tile_attend_evictscores_kernel(tc, query, keys_words, keys_scales, mass, dec
             nc.sync.dma_start(
                 scale_pool[row:P:QUADRANT, :].bitcast(I32), keys_scales[0, row::SCALE_ROWS, :].bitcast(I32)
             )
+        candidates = sb.tile([P, J // LIST_ROWS], U16)
+        nc.sync.dma_start(candidates[:], offs2)
         ones = held.tile([P, P], F32, offset=0)
         nc.vector.memset(ones[:], 1.0)
         identity = sb.tile([P, P], F32)

@@ -64,8 +64,8 @@ def tile_attend_evictscores_kernel(tc, query, keys_words, keys_scales, mass, dec
             )
         candidates = sb.tile([P, J // LIST_ROWS], U16)
         nc.sync.dma_start(candidates[:], offs2)
-        ones = held.tile([P, P], F32, offset=0)
-        nc.vector.memset(ones[:], 1.0)
+        ones = sb.tile([P, P], F32)
+        nc.gpsimd.memset(ones[:], 1.0)
         identity = sb.tile([P, P], F32)
         nc.gpsimd.affine_select(
             out=identity[:], in_=ones[:], pattern=[[-1, P]], compare_op=ALU.is_equal, fill=0.0, base=0,
@@ -134,8 +134,8 @@ def tile_attend_evictscores_kernel(tc, query, keys_words, keys_scales, mass, dec
         banks_lo = ps.tile([P, 3 * BANK], F32, offset=5 * BANK_BYTES)
         scores_lo = banks_lo[:, :H]
         scores_of(0, key_scales_lo, scores_lo)
-        bank_hi = ps.tile([P, H], F32, offset=0)
-        scores_hi = bank_hi[:]
+        banks_hi = ps.tile([P, 3 * BANK], F32, offset=0)
+        scores_hi = banks_hi[:, :H]
         scores_of(H, key_scales_hi, scores_hi)
 
         neg_max_lo = sb.tile([P, 1], F32)

@@ -17,8 +17,8 @@ FIRST_CREDIT_ROW = P - CREDIT_ROWS
 WEIGHT_SCALE = 512.0
 HEADROOM = 64.0
 H = I // 2
-SHARE = 448
-OWN_SCALED = 208
+SHARE = 384
+OWN_SCALED = 176
 TURNED = (1, 2, 3)
 FIRST_SLOTS = 160
 EARLY_SPREADS = 2
@@ -78,8 +78,8 @@ def tile_attend_evictscores_kernel(tc, query, keys_words, keys_scales, mass, dec
         mass_sb = late[:, :T]
         decay = late[:, T:]
         nc.sync.dma_start(decay, dec)
-        nc.sync.dma_start(mass_sb[:, BANK:], mass[:, BANK:])
-        nc.sync.dma_start(mass_sb[:, :BANK], mass[:, :BANK])
+        for k in TURNED + (0,):
+            nc.sync.dma_start(mass_sb[:, k * BANK : (k + 1) * BANK], mass[:, k * BANK : (k + 1) * BANK])
 
         credit_bank = ps.tile([P, BANK], F32, offset=6 * BANK_BYTES)
         nc.tensor.transpose(credit_bank[:, :P], credit_rows[:], identity[:])

@@ -189,8 +189,6 @@ def tile_attend_evictscores_kernel(tc, query, keys_words, keys_scales, mass, dec
                 )
 
         updated = held.tile([P, T], F32, offset=0)
-        rest = slice(SHARE, BANK)
-        nc.vector.scalar_tensor_tensor(updated[:, rest], placed[:, rest], row_factor[:], base_direct[:, rest], ALU.mult, ALU.add)
         placed_scaled = sb.tile([P, SHARE], F32)
         nc.gpsimd.tensor_scalar(
             placed_scaled[:, :OWN_SCALED], placed[:, :OWN_SCALED], row_factor[:], 0.0, ALU.mult, ALU.add
@@ -200,6 +198,8 @@ def tile_attend_evictscores_kernel(tc, query, keys_words, keys_scales, mass, dec
         for k in TURNED:
             cols = slice(k * BANK, (k + 1) * BANK)
             nc.vector.scalar_tensor_tensor(updated[:, cols], placed[:, cols], row_factor[:], base_banks[k][:], ALU.mult, ALU.add)
+        rest = slice(SHARE, BANK)
+        nc.vector.scalar_tensor_tensor(updated[:, rest], placed[:, rest], row_factor[:], base_direct[:, rest], ALU.mult, ALU.add)
         half_cand = J // 2 // LIST_ROWS
         picked_lo = sb.tile([P, J // 2], F32)
         nc.vector.tensor_tensor(picked_lo[:], updated[:].indirect(candidates[:, :half_cand]), twos[:], ALU.mult)

from contextlib import ExitStack

import concourse.mybir as mybir

D, T, I, J, Q = 512, 2048, 512, 256, 128
P = 128
PACK = 4
LIST_ROWS = 16
QUADRANT = 32
SCALE_ROWS = 4
BANK = 512
BLOCKS = BANK // P
QUARTERS = T // BANK
BANK_BYTES = 4 * BANK
CREDIT_ROWS = T // P
FIRST_CREDIT_ROW = P - CREDIT_ROWS
WEIGHT_SCALE = 512.0
HEADROOM = 64.0
H = I // 2
SHARE = 384
OWN_SCALED = 176
TURNED = (1, 2, 3)
FIRST_SLOTS = 160
EARLY_SPREADS = 2

F32 = mybir.dt.float32
BF16 = mybir.dt.bfloat16
I32 = mybir.dt.int32
U32 = mybir.dt.uint32
U16 = mybir.dt.uint16
U8 = mybir.dt.uint8
FP8X4 = mybir.dt.float8_e4m3fn_x4
FP4X4 = mybir.dt.float4_e2m1fn_x4
ALU = mybir.AluOpType
ACT = mybir.ActivationFunctionType
AXIS_X = mybir.AxisListType.X

FLOPS = 2 * D * Q * I


def tile_attend_evictscores_kernel(tc, query, keys_words, keys_scales, mass, dec, credit, offs, offs2, out):
    nc = tc.nc
    with ExitStack() as ctx:
        sb = ctx.enter_context(tc.tile_pool(name="sb", bufs=1))
        held = ctx.enter_context(tc.tile_pool(name="held", bufs=1))
        ps = ctx.enter_context(tc.psum_pool(name="ps", bufs=1))

        credit_rows = sb.tile([P, P], F32)
        nc.scalar.dma_start(credit_rows[FIRST_CREDIT_ROW:, :], credit.rearrange("o (c p) -> (o c) p", p=P))
        nc.gpsimd.memset(credit_rows[:FIRST_CREDIT_ROW, :], 0.0)
        minus_one = sb.tile([P, 1], F32, align_bytes=64, tag="query_bf")
        nc.gpsimd.memset(minus_one[:], -1.0)
        word_pool = sb.tile([P, T], U16, align_bytes=64, tag="word_pool")
        nc.sync.dma_start(word_pool[:].bitcast(I32), keys_words[0].bitcast(I32))
        slots = sb.tile([P, I // LIST_ROWS], U16)
        nc.sync.dma_start(slots[:], offs)
        query_raw = sb.tile([P, PACK, Q], F32, align_bytes=64, tag="query_raw")
        nc.sync.dma_start(query_raw[:], query.rearrange("(p j) q -> p j q", j=PACK))
        scale_pool = sb.tile([P, T], U8, align_bytes=64, tag="scale_pool")
        nc.vector.memset(scale_pool[:].bitcast(I32), 0)
        for row in range(SCALE_ROWS):
            nc.sync.dma_start(
                scale_pool[row:P:QUADRANT, :].bitcast(I32), keys_scales[0, row::SCALE_ROWS, :].bitcast(I32)
            )
        candidates = sb.tile([P, J // LIST_ROWS], U16)
        nc.sync.dma_start(candidates[:], offs2)
        ones = sb.tile([P, P], F32)
        nc.gpsimd.memset(ones[:], 1.0)
        identity = sb.tile([P, P], F32)
        nc.gpsimd.affine_select(
            out=identity[:], in_=ones[:], pattern=[[-1, P]], compare_op=ALU.is_equal, fill=0.0, base=0,
            channel_multiplier=1,
        )
        placed = sb.tile([P, T], F32)
        for k in range(QUARTERS):
            nc.vector.memset(placed[:, k * BANK : (k + 1) * BANK], 0.0)
        late = held.tile([P, T + 1], F32, offset=0)
        mass_sb = late[:, :T]
        decay = late[:, T:]
        nc.sync.dma_start(decay, dec)
        for k in TURNED + (0,):
            nc.sync.dma_start(mass_sb[:, k * BANK : (k + 1) * BANK], mass[:, k * BANK : (k + 1) * BANK])

        credit_bank = ps.tile([P, BANK], F32, offset=6 * BANK_BYTES)
        nc.tensor.transpose(credit_bank[:, :P], credit_rows[:], identity[:])
        debit = sb.tile([P, CREDIT_ROWS], F32)
        nc.scalar.mul(debit[:], credit_bank[:, FIRST_CREDIT_ROW:P], minus_one[:])
        base_banks = {}

        def spread_debit(k, bank):
            base_bank = ps.tile([P, BANK], F32, offset=bank * BANK_BYTES, name="base_bank%d" % k)
            for i in range(BLOCKS):
                c = k * BLOCKS + i
                nc.tensor.matmul(
                    base_bank[:, i * P : (i + 1) * P], debit[:, c : c + 1].to_broadcast([P, P]), identity[:],
                    is_transpose=True, start=i == 0, stop=k == 0 and i == BLOCKS - 1,
                )
            base_banks[k] = base_bank

        for k in range(EARLY_SPREADS):
            spread_debit(k, 3 + k)

        half_list = H // LIST_ROWS
        key_words = sb.tile([P, I], U16, align_bytes=64)
        nc.vector.tensor_copy(key_words[:], word_pool[:].indirect(slots[:]))
        key_scales_lo = sb.tile([P, H], U8, align_bytes=64)
        nc.vector.tensor_copy(key_scales_lo[:], scale_pool[:].indirect(slots[:, :half_list]))
        query_bf = sb.tile([P, Q, PACK], BF16, align_bytes=64, tag="query_bf")
        nc.scalar.copy(
            query_bf[:].rearrange("p (c i) j -> p c j i", i=PACK),
            query_raw[:].rearrange("p j (c i) -> p c j i", i=PACK),
        )
        query_codes = sb.tile([P, Q], U32, align_bytes=64, tag="word_pool")
        query_scales = sb.tile([P, Q], U8, align_bytes=64)
        nc.vector.quantize_mx(
            out=query_codes[:].bitcast(FP8X4),
            scales=query_scales[:],
            in_=query_bf[:].rearrange("p q j -> p (q j)"),
        )
        key_scales_hi = sb.tile([P, H], U8, align_bytes=64, tag="query_raw")
        nc.vector.tensor_copy(key_scales_hi[:], scale_pool[:].indirect(slots[:, half_list:]))

        def scores_of(first, key_scales, scores):
            nc.tensor.matmul_mx(
                out=scores,
                lhsT=query_codes[:].bitcast(FP8X4),
                lhsT_scale=query_scales[:],
                rhs=key_words[:, first : first + H].bitcast(FP4X4),
                rhs_scale=key_scales[:],
                start=True,
                stop=True,
            )

        banks_lo = ps.tile([P, 3 * BANK], F32, offset=5 * BANK_BYTES)
        scores_lo = banks_lo[:, :H]
        scores_of(0, key_scales_lo, scores_lo)
        banks_hi = ps.tile([P, 3 * BANK], F32, offset=0)
        scores_hi = banks_hi[:, :H]
        scores_of(H, key_scales_hi, scores_hi)

        neg_max_lo = sb.tile([P, 1], F32)
        nc.vector.tensor_reduce(neg_max_lo[:], scores_lo, AXIS_X, ALU.max, negate=True)
        above_hi = sb.tile([P, H], F32)
        reach_hi = sb.tile([P, 1], F32, tag="reach_hi")
        nc.vector.tensor_scalar(above_hi[:], scores_hi, neg_max_lo[:], HEADROOM, ALU.add, ALU.max, accum_out=reach_hi[:])
        weights = sb.tile([P, I], F32)
        part_sums = sb.tile([P, 3], F32)
        for i, part in enumerate((slice(0, FIRST_SLOTS), slice(FIRST_SLOTS, H))):
            nc.scalar.activation(
                weights[:, part], scores_lo[:, part], ACT.Exp, bias=neg_max_lo[:], accum_out=part_sums[:, i : i + 1]
            )
        neg_excess_hi = sb.tile([P, 1], F32)
        nc.scalar.activation(neg_excess_hi[:], reach_hi[:], ACT.Copy, bias=HEADROOM, scale=-1.0)
        nc.scalar.activation(weights[:, H:], above_hi[:], ACT.Exp, bias=neg_excess_hi[:], accum_out=part_sums[:, 2:])
        twos = sb.tile([P, J // 2], F32, align_bytes=64, tag="scale_pool")
        nc.gpsimd.memset(twos[:], 2.0)
        first_cols = FIRST_SLOTS // LIST_ROWS
        nc.vector.tensor_tensor(placed[:].indirect(slots[:, :first_cols]), weights[:, :FIRST_SLOTS], weights[:, :FIRST_SLOTS], ALU.add)
        nc.scalar.activation(placed[:].indirect(slots[:, first_cols:]), weights[:, FIRST_SLOTS:], ACT.Copy, scale=2.0)
        row_sum_scaled = sb.tile([P, 1], F32)
        part_sums_scaled = sb.tile([P, 3], F32)
        nc.vector.tensor_scalar(
            part_sums_scaled[:], part_sums[:], 2.0 / WEIGHT_SCALE, None, ALU.mult, ALU.add, accum_out=row_sum_scaled[:]
        )
        row_factor = sb.tile([P, 1], F32)
        nc.vector.reciprocal(row_factor[:], row_sum_scaled[:])

        decay_bank = ps.tile([P, BANK], F32, offset=7 * BANK_BYTES)
        nc.tensor.transpose(decay_bank[:, :P], decay.to_broadcast([P, P]), identity[:])
        decay_row = sb.tile([P, 1, P], F32)
        nc.vector.tensor_copy(decay_row[:, 0, :], decay_bank[:, :P])
        base_direct = sb.tile([P, BANK], F32, tag="reach_hi")
        nc.vector.scalar_tensor_tensor(base_direct[:], mass_sb[:, :BANK], decay, base_banks[0][:], ALU.mult, ALU.add)
        turned_banks = {}
        for k in TURNED:
            turned_banks[k] = ps.tile([P, BLOCKS, P], F32, offset=k % 3 * BANK_BYTES, name="turned%d" % k)
            for i in range(BLOCKS):
                first = k * BANK + i * P
                nc.tensor.transpose(turned_banks[k][:, i, :], mass_sb[:, first : first + P], identity[:])
        for k in range(EARLY_SPREADS, QUARTERS):
            spread_debit(k, 3 + k)
        for k in TURNED:
            base_turned = sb.tile([P, BLOCKS, P], F32, name="base_turned%d" % k)
            nc.vector.tensor_tensor(base_turned[:], decay_row[:].to_broadcast([P, BLOCKS, P]), turned_banks[k][:], ALU.mult)
            for i in range(BLOCKS):
                nc.tensor.matmul(
                    base_banks[k][:, i * P : (i + 1) * P], base_turned[:, i, :], identity[:],
                    is_transpose=True, start=False, stop=i == BLOCKS - 1,
                )

        updated = held.tile([P, T], F32, offset=0)
        placed_scaled = sb.tile([P, SHARE], F32)
        nc.gpsimd.tensor_scalar(
            placed_scaled[:, :OWN_SCALED], placed[:, :OWN_SCALED], row_factor[:], 0.0, ALU.mult, ALU.add
        )
        nc.scalar.mul(placed_scaled[:, OWN_SCALED:], placed[:, OWN_SCALED:SHARE], row_factor[:])
        nc.gpsimd.tensor_tensor(updated[:, :SHARE], placed_scaled[:], base_direct[:, :SHARE], ALU.add)
        for k in TURNED:
            cols = slice(k * BANK, (k + 1) * BANK)
            nc.vector.scalar_tensor_tensor(updated[:, cols], placed[:, cols], row_factor[:], base_banks[k][:], ALU.mult, ALU.add)
        rest = slice(SHARE, BANK)
        nc.vector.scalar_tensor_tensor(updated[:, rest], placed[:, rest], row_factor[:], base_direct[:, rest], ALU.mult, ALU.add)
        half_cand = J // 2 // LIST_ROWS
        picked_lo = sb.tile([P, J // 2], F32)
        nc.vector.tensor_tensor(picked_lo[:], updated[:].indirect(candidates[:, :half_cand]), twos[:], ALU.mult)
        nc.sync.dma_start(out[:, : J // 2], picked_lo[:])
        picked_hi = sb.tile([P, J // 2], F32)
        nc.scalar.activation(picked_hi[:], updated[:].indirect(candidates[:, half_cand:]), ACT.Copy, scale=2.0)
        nc.scalar.dma_start(out[:, J // 2 :], picked_hi[:])
